import numpy as np
import ml_dtypes


def mxq(x, axis, fmt="e4m3"):
    dtype, down = {"e4m3": (ml_dtypes.float8_e4m3fn, 7), "e5m2": (ml_dtypes.float8_e5m2, 14)}[fmt]
    v = np.moveaxis(np.asarray(x, np.float32).astype(ml_dtypes.bfloat16).astype(np.float64), axis, -1)
    blocks = v.reshape(v.shape[:-1] + (-1, 32))
    amax = np.abs(blocks).max(-1, keepdims=True)
    byte = np.maximum(np.where(amax > 0, np.frexp(amax)[1] - 1 + 127, 0) - down, 1)
    scale = np.exp2(byte - 127.0)
    codes = (blocks / scale).astype(np.float32).astype(dtype).astype(np.float64)
    return np.moveaxis((codes * scale).reshape(v.shape), -1, axis)


WIDE = False


def mx_kscale(k):
    if not WIDE:
        return np.ones(k)
    levels = np.array([10, -10, 5, -5, 0])
    if k % 512:
        return np.exp2(np.random.permutation(np.resize(levels, k // 32))).repeat(32)
    a = np.empty((k // 512, 16))
    for p in range(k // 512):
        a[p, :8] = np.random.permutation(np.resize(levels, 8))
        for g in range(8):
            far = levels[np.abs(levels - a[p, g]) >= 10]
            a[p, g + 8] = far[np.random.randint(len(far))]
    return np.exp2(a.ravel()).repeat(32)


def f64(x):
    return np.asarray(x).astype(np.float64)


def striped(idx):
    return np.tile(idx.reshape(-1, 16).T, (8, 1)).astype(np.uint16)


def unstriped(offs):
    return offs[:16].T.reshape(-1).astype(np.int64)


K, T, D, V, H, N = 2048, 512, 6, 256, 512, 128
P = 2 ** 7


def setup_inputs():
    n = np.random.standard_normal
    s = mx_kscale(K)[:, None]
    u = mx_kscale(H)
    return {
        "xT": (n((K, T)) * s).astype(np.float32),
        "w1": (n((K, H)) / np.sqrt(K) / s * u).astype(np.float32),
        "w2": (n((H, N)) / np.sqrt(H) / u[:, None]).astype(np.float32),
        "gate": np.tile(np.random.uniform(0.2, 1.0, (D, 1, V)) / np.sqrt(D), (1, P, 1)).astype(np.float32),
        "pos1": striped(np.random.permutation(T)[:V]),
        "pos2": striped(np.random.permutation(T)[:V]),
        "pos3": striped(np.random.permutation(T)[:V]),
        "pos4": striped(np.random.permutation(T)[:V]),
        "pos5": striped(np.random.permutation(T)[:V]),
        "pos6": striped(np.random.permutation(T)[:V]),
    }


def reference(xT, w1, w2, gate, pos1, pos2, pos3, pos4, pos5, pos6):
    h = mxq(f64(w1), 0, "e4m3").T @ mxq(f64(xT), 0, "e4m3")
    z = sum(f64(gate)[d, :1] * h[:, unstriped(p)] for d, p in enumerate((pos1, pos2, pos3, pos4, pos5, pos6)))
    return mxq(f64(w2), 0, "e4m3").T @ mxq(z, 0, "e4m3")

@@ -1,0 +1,247 @@
+from contextlib import ExitStack
+
+import concourse.mybir as mybir
+from concourse.masks import make_identity
+
+K, T, D, V, H, N = 2048, 512, 6, 256, 512, 128
+P = 128
+PASSES = K // 512
+BLOCKS = H // P
+HALVES = V // P
+FLOPS = 2 * K * H * T + 2 * H * N * V
+BYTES = 4 * (K * T + K * H + H * N + D * V + N * V) + 2 * D * P * (V // 16)
+
+F32 = mybir.dt.float32
+BF16 = mybir.dt.bfloat16
+U32 = mybir.dt.uint32
+U16 = mybir.dt.uint16
+U8 = mybir.dt.uint8
+FP8X4 = mybir.dt.float8_e4m3fn_x4
+MULT = mybir.AluOpType.mult
+
+
+def tile_picked_gcn_mlp_none_sub_l_kernel(tc, xT, w1, w2, gate, pos1, pos2, pos3, pos4, pos5, pos6, out):
+    nc = tc.nc
+    lists_in = (pos1, pos2, pos3, pos4, pos5, pos6)
+
+    with ExitStack() as ctx:
+        lists = ctx.enter_context(tc.tile_pool(name="lists", bufs=1))
+        keep = ctx.enter_context(tc.tile_pool(name="keep", bufs=1))
+        turns = ctx.enter_context(tc.tile_pool(name="turns", bufs=1))
+        psum = ctx.enter_context(tc.psum_pool(name="psum", bufs=2))
+        psum1 = ctx.enter_context(tc.psum_pool(name="psum1", bufs=1))
+
+        pos = [lists.tile([P, V // 16], U16, name=f"pos{d}") for d in range(D)]
+
+        xraw = [keep.tile([P, 4, T], F32, name=f"xraw{c}") for c in range(PASSES)]
+        wraw = [[keep.tile([P, 2, 4, P], F32, name=f"wraw{b}_{s}") for s in range(2)] for b in range(BLOCKS)]
+        w2raw = keep.tile([P, 4, N], F32, name="w2raw")
+        gate_rows = keep.tile([P, P], F32, name="gate_rows")
+        nc.gpsimd.memset(gate_rows[:], 0.0)
+
+        def load_w1(b, c):
+            nc.sync.dma_start(
+                out=wraw[b][c // 2][:, c % 2, :, :],
+                in_=w1[512 * c : 512 * (c + 1), P * b : P * (b + 1)].rearrange("(p j) w -> p j w", j=4),
+            )
+
+        def load_list(d):
+            nc.sync.dma_start(pos[d][:], lists_in[d])
+
+        for c in range(PASSES):
+            nc.sync.dma_start(out=xraw[c][:], in_=xT[512 * c : 512 * (c + 1), :].rearrange("(p j) w -> p j w", j=4))
+            if c == 0:
+                for v in range(HALVES):
+                    nc.sync.dma_start(out=gate_rows[D * v : D * (v + 1), :], in_=gate[:, 0, P * v : P * (v + 1)])
+        for c in range(PASSES):
+            load_w1(0, c)
+        load_list(0)
+        load_list(1)
+        load_w1(1, 0)
+        load_list(2)
+        load_w1(1, 1)
+        load_list(3)
+        load_w1(1, 2)
+        load_list(4)
+        load_list(5)
+        load_w1(1, 3)
+        for c in range(PASSES):
+            load_w1(2, c)
+        nc.sync.dma_start(out=w2raw[:], in_=w2.rearrange("(p j) m -> p j m", j=4))
+        for c in range(PASSES):
+            load_w1(3, c)
+
+        ident = keep.tile([P, P], F32, name="ident")
+        make_identity(nc, ident[:])
+
+        def spread_gates():
+            gate_bank = psum.tile([P, T], F32, name="bank")
+            nc.tensor.transpose(gate_bank[:, :P], gate_rows[:], ident[:])
+            gate_cols = keep.tile([P, D * HALVES], F32, name="gate_cols")
+            nc.vector.tensor_copy(gate_cols[:], gate_bank[:, : D * HALVES])
+            gates = []
+            for g in range(D // 2):
+                gate_bank = psum.tile([P, T], F32, name="bank")
+                for e in range(2):
+                    for v in range(HALVES):
+                        j = D * v + 2 * g + e
+                        nc.tensor.transpose(
+                            gate_bank[:, (2 * e + v) * P : (2 * e + v + 1) * P],
+                            gate_cols[:, j : j + 1].to_broadcast([P, P]),
+                            ident[:],
+                        )
+                pair = keep.tile([P, 2, V], F32, name=f"gates{g}")
+                nc.scalar.copy(pair[:].rearrange("p e v -> p (e v)"), gate_bank[:])
+                gates.append(pair)
+            return gates
+
+        xq = []
+        for c in range(PASSES):
+            grouped = keep.tile([P, T, 4], BF16, name=f"xg{c}", align_bytes=64)
+            codes = keep.tile([P, T], U32, name=f"xq{c}", align_bytes=64)
+            scales = keep.tile([P, T], U8, name=f"xs{c}", align_bytes=64)
+            cut = 160
+            nc.scalar.copy(
+                grouped[:, :cut, :].rearrange("p (c i) t -> p c t i", i=4),
+                xraw[c][:, :, :cut].rearrange("p t (c i) -> p c t i", i=4),
+            )
+            nc.vector.tensor_copy(
+                grouped[:, cut:, :].rearrange("p (c i) t -> p c t i", i=4),
+                xraw[c][:, :, cut:].rearrange("p t (c i) -> p c t i", i=4),
+            )
+            nc.vector.quantize_mx(out=codes[:].bitcast(FP8X4), scales=scales[:], in_=grouped[:].rearrange("p w t -> p (w t)"))
+            xq.append((codes, scales))
+            if c == 1:
+                gates = spread_gates()
+
+        wq = {}
+        h = [keep.tile([P, T], F32, name=f"h{b}") for b in range(BLOCKS)]
+
+        def multiply(bank, b, c, nodes):
+            nc.tensor.matmul_mx(
+                out=bank,
+                lhsT=wq[b, c][0].bitcast(FP8X4),
+                lhsT_scale=wq[b, c][1],
+                rhs=xq[c][0][:, nodes].bitcast(FP8X4),
+                rhs_scale=xq[c][1][:, nodes],
+                start=(c == 0),
+                stop=(c == PASSES - 1),
+            )
+
+        bank = psum.tile([P, T], F32, name="bank")
+        def interleave(copy, grouped, b, c, columns):
+            copy(
+                grouped[:, columns, :].rearrange("p (c i) t -> p c t i", i=4),
+                wraw[b][c // 2][:, c % 2, :, columns].rearrange("p t (c i) -> p c t i", i=4),
+            )
+
+        def quantise_w1(grouped, b, passes):
+            n = len(passes)
+            codes = keep.tile([P, n, P], U32, name=f"wq{b}_{passes[0]}", align_bytes=64)
+            scales = keep.tile([P, n, P], U8, name=f"ws{b}_{passes[0]}", align_bytes=64)
+            nc.vector.quantize_mx(
+                out=codes[:].rearrange("p c w -> p (c w)").bitcast(FP8X4),
+                scales=scales[:].rearrange("p c w -> p (c w)"),
+                in_=grouped.rearrange("p c w t -> p (c w t)"),
+            )
+            for e, c in enumerate(passes):
+                wq[b, c] = (codes[:, e, :], scales[:, e, :])
+
+        for c in range(PASSES):
+            grouped = keep.tile([P, 1, P, 4], BF16, name=f"wg{c}", align_bytes=64)
+            interleave(nc.scalar.copy, grouped[:, 0], 0, c, slice(0, 64))
+            interleave(nc.vector.tensor_copy, grouped[:, 0], 0, c, slice(64, P))
+            quantise_w1(grouped[:], 0, (c,))
+            multiply(bank[:], 0, c, slice(0, T))
+        nc.vector.tensor_copy(h[0][:], bank[:])
+
+        w2g = keep.tile([P, N, 4], BF16, name="w2g", align_bytes=64)
+        w2q = keep.tile([P, N], U32, name="w2q", align_bytes=64)
+        w2s = keep.tile([P, N], U8, name="w2s", align_bytes=64)
+        zT = [keep.tile([P, 2, P, 2], BF16, name=f"zT{v}") for v in range(HALVES)]
+
+        def gather(b, d, targets, picked):
+            nc.vector.tensor_tensor(
+                picked, h[b][:].indirect(pos[d][:, targets.start // 16 : targets.stop // 16]), gates[d // 2][:, d % 2, targets], MULT
+            )
+
+        def add_turned(acc, picked, d):
+            nc.tensor.matmul(acc, picked, ident[:], is_transpose=True, start=(d == 0), stop=(d == D - 1))
+
+        def round_sums(copy, b, v, acc):
+            copy(zT[v][:, :, 32 * b : 32 * (b + 1), :], acc.rearrange("r (q u e) -> r u q e", u=2, e=2))
+
+        parts = {b: (((0, 1), 0), ((2, 3), 1)) for b in (1, 2, 3)}
+        for b in range(BLOCKS - 1):
+            waiting = {}
+            for k, (passes, d) in enumerate(parts[b + 1]):
+                grouped = turns.tile([P, len(passes), P, 4], BF16, name=f"turn{b}_{k}", align_bytes=64)
+                for e, c in enumerate(passes):
+                    interleave(nc.scalar.copy, grouped[:, e], b + 1, c, slice(0, P))
+                waiting[d] = (k, passes, grouped)
+            bank = psum.tile([P, T], F32, name="bank")
+            acc = [psum.tile([P, P], F32, name=f"acc{v}") for v in range(HALVES)]
+            for d in range(D):
+                if d in waiting:
+                    k, passes, grouped = waiting[d]
+                    quantise_w1(grouped[:], b + 1, passes)
+                    for c in passes:
+                        multiply(bank[:], b + 1, c, slice(0, T))
+                    if passes[-1] == PASSES - 1:
+                        nc.scalar.copy(h[b + 1][:], bank[:])
+                    picked = turns.tile([P, V], F32, name=f"turn{b}_{k}", align_bytes=64)
+                else:
+                    picked = keep.tile([P, V], F32, name=f"picked{b}_{d}")
+                gather(b, d, slice(0, V), picked[:])
+                for v in range(HALVES):
+                    add_turned(acc[v][:], picked[:, P * v : P * (v + 1)], d)
+            for v in range(HALVES):
+                round_sums(nc.scalar.copy, b, v, acc[v][:])
+            if b == 1:
+                nc.scalar.copy(w2g[:], w2raw[:].rearrange("p t m -> p m t"))
+            if b == 2:
+                nc.vector.quantize_mx(out=w2q[:].bitcast(FP8X4), scales=w2s[:], in_=w2g[:].rearrange("p m t -> p (m t)"))
+
+        b = BLOCKS - 1
+        zbank = [psum1.tile([P, 2, P], F32, name=f"zbank{v}") for v in range(HALVES)]
+        zg = [keep.tile([P, P, 4], BF16, name=f"zg{v}", align_bytes=64) for v in range(HALVES)]
+        zq = [keep.tile([P, P], U32, name=f"zq{v}", align_bytes=64) for v in range(HALVES)]
+        zs = [keep.tile([P, P], U8, name=f"zs{v}", align_bytes=64) for v in range(HALVES)]
+        result = [keep.tile([P, P], F32, name=f"result{v}") for v in range(HALVES)]
+        acc = [psum.tile([P, P], F32, name=f"acc{v}") for v in range(HALVES)]
+
+        def pick_half(v):
+            for d in range(D):
+                picked = keep.tile([P, P], F32, name=f"picked{b}_{d}_{v}")
+                gather(b, d, slice(P * v, P * (v + 1)), picked[:])
+                add_turned(acc[v][:], picked[:], d)
+
+        def turn_back(v):
+            words = zT[v][:].rearrange("r u p e -> r (u p e)").bitcast(F32)
+            for u in range(2):
+                nc.tensor.transpose(zbank[v][:, u, :], words[:, P * u : P * (u + 1)], ident[:])
+            nc.scalar.copy(
+                zg[v][:].rearrange("p r t -> p (r t)").bitcast(F32).rearrange("p (r u) -> p r u", u=2),
+                zbank[v][:].rearrange("p u r -> p r u"),
+            )
+
+        def second_layer(v, copy, queue):
+            nc.vector.quantize_mx(out=zq[v][:].bitcast(FP8X4), scales=zs[v][:], in_=zg[v][:].rearrange("p r t -> p (r t)"))
+            bank = psum.tile([P, T], F32, name="bank")
+            nc.tensor.matmul_mx(
+                out=bank[:, :P],
+                lhsT=w2q[:].bitcast(FP8X4), lhsT_scale=w2s[:],
+                rhs=zq[v][:].bitcast(FP8X4), rhs_scale=zs[v][:],
+                start=True, stop=True,
+            )
+            copy(result[v][:], bank[:, :P])
+            queue.dma_start(out=out[:, P * v : P * (v + 1)], in_=result[v][:])
+
+        pick_half(0)
+        round_sums(nc.scalar.copy, b, 0, acc[0][:])
+        turn_back(0)
+        pick_half(1)
+        second_layer(0, nc.scalar.copy, nc.sync)
+        round_sums(nc.vector.tensor_copy, b, 1, acc[1][:])
+        turn_back(1)
+        second_layer(1, nc.vector.tensor_copy, nc.sync)

@@ -28,33 +28,41 @@ def tile_picked_gcn_mlp_none_sub_l_kernel(tc, xT, w1, w2, gate, pos1, pos2, pos3
         lists = ctx.enter_context(tc.tile_pool(name="lists", bufs=1))
         keep = ctx.enter_context(tc.tile_pool(name="keep", bufs=1))
         turns = ctx.enter_context(tc.tile_pool(name="turns", bufs=1))
-        psum = ctx.enter_context(tc.psum_pool(name="psum", bufs=2))
-        psum1 = ctx.enter_context(tc.psum_pool(name="psum1", bufs=1))
+        psum = ctx.enter_context(tc.psum_pool(name="psum", bufs=1))
 
         pos = [lists.tile([P, V // 16], U16, name=f"pos{d}") for d in range(D)]
 
-        xraw = [keep.tile([P, 4, T], F32, name=f"xraw{c}") for c in range(PASSES)]
-        wraw = [[keep.tile([P, 2, 4, P], F32, name=f"wraw{b}_{s}") for s in range(2)] for b in range(BLOCKS)]
+        LAST = PASSES - 1
+        HT = T // 2
+        xraw = [turns.tile([P, 4, T], F32, name=f"xraw{c}", align_bytes=64) for c in range(LAST)]
+        xlast = [turns.tile([P, 4, HT], F32, name=f"xlast{a}", align_bytes=64) for a in range(2)]
+        wraw = [[turns.tile([P, 4, P], F32, name=f"wraw{b}_{c}", align_bytes=64) for c in range(PASSES)] for b in range(BLOCKS)]
         w2raw = keep.tile([P, 4, N], F32, name="w2raw")
-        gate_rows = keep.tile([P, P], F32, name="gate_rows")
-        nc.gpsimd.memset(gate_rows[:], 0.0)
+        gate_rows = keep.tile([P, V], F32, name="gate_rows")
+        nc.gpsimd.memset(gate_rows[: P - D, :], 0.0)
 
         def load_w1(b, c):
             nc.sync.dma_start(
-                out=wraw[b][c // 2][:, c % 2, :, :],
+                out=wraw[b][c][:],
                 in_=w1[512 * c : 512 * (c + 1), P * b : P * (b + 1)].rearrange("(p j) w -> p j w", j=4),
             )
 
         def load_list(d):
             nc.sync.dma_start(pos[d][:], lists_in[d])
 
-        for c in range(PASSES):
-            nc.sync.dma_start(out=xraw[c][:], in_=xT[512 * c : 512 * (c + 1), :].rearrange("(p j) w -> p j w", j=4))
-            if c == 0:
-                for v in range(HALVES):
-                    nc.sync.dma_start(out=gate_rows[D * v : D * (v + 1), :], in_=gate[:, 0, P * v : P * (v + 1)])
-        for c in range(PASSES):
+        for c in range(2):
             load_w1(0, c)
+            if c == 0:
+                nc.sync.dma_start(out=gate_rows[P - D : P - D + 4, :], in_=gate[0:4, 0, :])
+                nc.sync.dma_start(out=gate_rows[P - 2 :, :], in_=gate[4:6, 0, :])
+        for c in range(LAST):
+            nc.sync.dma_start(out=xraw[c][:], in_=xT[512 * c : 512 * (c + 1), :].rearrange("(p j) w -> p j w", j=4))
+        load_w1(0, 2)
+        load_w1(0, 3)
+        for a in range(2):
+            nc.sync.dma_start(
+                out=xlast[a][:], in_=xT[512 * LAST :, HT * a : HT * (a + 1)].rearrange("(p j) w -> p j w", j=4)
+            )
         load_list(0)
         load_list(1)
         load_w1(1, 0)
@@ -65,57 +73,61 @@ def tile_picked_gcn_mlp_none_sub_l_kernel(tc, xT, w1, w2, gate, pos1, pos2, pos3
         load_list(4)
         load_list(5)
         load_w1(1, 3)
-        for c in range(PASSES):
-            load_w1(2, c)
+        for b in (2, 3):
+            for c in range(PASSES):
+                load_w1(b, c)
         nc.sync.dma_start(out=w2raw[:], in_=w2.rearrange("(p j) m -> p j m", j=4))
-        for c in range(PASSES):
-            load_w1(3, c)
 
         ident = keep.tile([P, P], F32, name="ident")
         make_identity(nc, ident[:])
 
         def spread_gates():
-            gate_bank = psum.tile([P, T], F32, name="bank")
-            nc.tensor.transpose(gate_bank[:, :P], gate_rows[:], ident[:])
-            gate_cols = keep.tile([P, D * HALVES], F32, name="gate_cols")
-            nc.vector.tensor_copy(gate_cols[:], gate_bank[:, : D * HALVES])
+            gate_bank = psum.tile([P, T], F32, name="zbank0")
+            for v in range(HALVES):
+                nc.tensor.transpose(gate_bank[:, P * v : P * (v + 1)], gate_rows[:, P * v : P * (v + 1)], ident[:])
+            gate_cols = turns.tile([P, HALVES, 8], F32, name="xg", align_bytes=64)
+            nc.vector.tensor_copy(gate_cols[:], gate_bank[:, :V].rearrange("p (v r) -> p v r", v=HALVES)[:, :, P - 8 :])
             gates = []
             for g in range(D // 2):
-                gate_bank = psum.tile([P, T], F32, name="bank")
+                gate_bank = psum.tile([P, T], F32, name=("zbank1", "last0", "last1")[g])
                 for e in range(2):
                     for v in range(HALVES):
-                        j = D * v + 2 * g + e
+                        d = 2 * g + e
                         nc.tensor.transpose(
                             gate_bank[:, (2 * e + v) * P : (2 * e + v + 1) * P],
-                            gate_cols[:, j : j + 1].to_broadcast([P, P]),
+                            gate_cols[:, v, 2 + d : 3 + d].to_broadcast([P, P]),
                             ident[:],
                         )
                 pair = keep.tile([P, 2, V], F32, name=f"gates{g}")
-                nc.scalar.copy(pair[:].rearrange("p e v -> p (e v)"), gate_bank[:])
+                (nc.vector.tensor_copy if g == 1 else nc.scalar.copy)(pair[:].rearrange("p e v -> p (e v)"), gate_bank[:])
                 gates.append(pair)
             return gates
 
-        xq = []
-        for c in range(PASSES):
-            grouped = keep.tile([P, T, 4], BF16, name=f"xg{c}", align_bytes=64)
-            codes = keep.tile([P, T], U32, name=f"xq{c}", align_bytes=64)
-            scales = keep.tile([P, T], U8, name=f"xs{c}", align_bytes=64)
-            cut = 160
-            nc.scalar.copy(
-                grouped[:, :cut, :].rearrange("p (c i) t -> p c t i", i=4),
-                xraw[c][:, :, :cut].rearrange("p t (c i) -> p c t i", i=4),
-            )
-            nc.vector.tensor_copy(
-                grouped[:, cut:, :].rearrange("p (c i) t -> p c t i", i=4),
-                xraw[c][:, :, cut:].rearrange("p t (c i) -> p c t i", i=4),
-            )
-            nc.vector.quantize_mx(out=codes[:].bitcast(FP8X4), scales=scales[:], in_=grouped[:].rearrange("p w t -> p (w t)"))
-            xq.append((codes, scales))
-            if c == 1:
-                gates = spread_gates()
+        def interleave(copy, grouped, raw):
+            copy(grouped.rearrange("p (c i) t -> p c t i", i=4), raw.rearrange("p t (c i) -> p c t i", i=4))
 
         wq = {}
-        h = [keep.tile([P, T], F32, name=f"h{b}") for b in range(BLOCKS)]
+
+        def quantise_w1(grouped, b, passes):
+            n = len(passes)
+            codes = turns.tile([P, n, P], U32, name=f"wq{b}_{passes[0]}", align_bytes=64)
+            scales = keep.tile([P, n, P], U8, name=f"ws{b}_{passes[0]}", align_bytes=64)
+            nc.vector.quantize_mx(
+                out=codes[:].rearrange("p c w -> p (c w)").bitcast(FP8X4),
+                scales=scales[:].rearrange("p c w -> p (c w)"),
+                in_=grouped.rearrange("p c w t -> p (c w t)"),
+            )
+            for e, c in enumerate(passes):
+                wq[b, c] = (codes[:, e, :], scales[:, e, :])
+
+        xq = [
+            (
+                keep.tile([P, T], U32, name=f"xq{c}", align_bytes=64),
+                keep.tile([P, T], U8, name=f"xs{c}", align_bytes=64),
+            )
+            for c in range(PASSES)
+        ]
+        h = {0: keep.tile([P, T], F32, name="h0")}
 
         def multiply(bank, b, c, nodes):
             nc.tensor.matmul_mx(
@@ -128,34 +140,37 @@ def tile_picked_gcn_mlp_none_sub_l_kernel(tc, xT, w1, w2, gate, pos1, pos2, pos3
                 stop=(c == PASSES - 1),
             )
 
-        bank = psum.tile([P, T], F32, name="bank")
-        def interleave(copy, grouped, b, c, columns):
-            copy(
-                grouped[:, columns, :].rearrange("p (c i) t -> p c t i", i=4),
-                wraw[b][c // 2][:, c % 2, :, columns].rearrange("p t (c i) -> p c t i", i=4),
-            )
-
-        def quantise_w1(grouped, b, passes):
-            n = len(passes)
-            codes = keep.tile([P, n, P], U32, name=f"wq{b}_{passes[0]}", align_bytes=64)
-            scales = keep.tile([P, n, P], U8, name=f"ws{b}_{passes[0]}", align_bytes=64)
+        def quantise_x(c, raw, nodes, cut, name):
+            width = nodes.stop - nodes.start
+            grouped = turns.tile([P, width, 4], BF16, name=name, align_bytes=64)
+            interleave(nc.scalar.copy, grouped[:, :cut, :], raw[:, :, :cut])
+            interleave(nc.vector.tensor_copy, grouped[:, cut:, :], raw[:, :, cut:])
             nc.vector.quantize_mx(
-                out=codes[:].rearrange("p c w -> p (c w)").bitcast(FP8X4),
-                scales=scales[:].rearrange("p c w -> p (c w)"),
-                in_=grouped.rearrange("p c w t -> p (c w t)"),
+                out=xq[c][0][:, nodes].bitcast(FP8X4), scales=xq[c][1][:, nodes], in_=grouped[:].rearrange("p w t -> p (w t)")
             )
-            for e, c in enumerate(passes):
-                wq[b, c] = (codes[:, e, :], scales[:, e, :])
 
-        for c in range(PASSES):
-            grouped = keep.tile([P, 1, P, 4], BF16, name=f"wg{c}", align_bytes=64)
-            interleave(nc.scalar.copy, grouped[:, 0], 0, c, slice(0, 64))
-            interleave(nc.vector.tensor_copy, grouped[:, 0], 0, c, slice(64, P))
-            quantise_w1(grouped[:], 0, (c,))
-            multiply(bank[:], 0, c, slice(0, T))
-        nc.vector.tensor_copy(h[0][:], bank[:])
+        grouped = keep.tile([P, 2, P, 4], BF16, name="wg0", align_bytes=64)
+        interleave(nc.scalar.copy, grouped[:, 0], wraw[0][0][:])
+        interleave(nc.vector.tensor_copy, grouped[:, 1], wraw[0][1][:])
+        quantise_w1(grouped[:], 0, (0, 1))
+        gates = spread_gates()
+        first = [psum.tile([P, HT], F32, name=f"hbank{a}") for a in range(2)]
+        halves = [slice(HT * a, HT * (a + 1)) for a in range(2)]
+        for c in range(LAST):
+            quantise_x(c, xraw[c], slice(0, T), 176, "xg")
+            if c == 2:
+                grouped = turns.tile([P, 2, P, 4], BF16, name="xraw2", align_bytes=64)
+                interleave(nc.scalar.copy, grouped[:, 0], wraw[0][2][:])
+                interleave(nc.vector.tensor_copy, grouped[:, 1], wraw[0][3][:])
+                quantise_w1(grouped[:], 0, (2, 3))
+            for a in range(2):
+                multiply(first[a][:], 0, c, halves[a])
+        for a in range(2):
+            quantise_x(LAST, xlast[a], halves[a], (128, 80)[a], ("xg", "xlast0")[a])
+            multiply(first[a][:], 0, LAST, halves[a])
+        nc.scalar.copy(h[0][:, halves[0]], first[0][:])
+        nc.vector.tensor_copy(h[0][:, halves[1]], first[1][:])
 
-        w2g = keep.tile([P, N, 4], BF16, name="w2g", align_bytes=64)
         w2q = keep.tile([P, N], U32, name="w2q", align_bytes=64)
         w2s = keep.tile([P, N], U8, name="w2s", align_bytes=64)
         zT = [keep.tile([P, 2, P, 2], BF16, name=f"zT{v}") for v in range(HALVES)]
@@ -168,19 +183,23 @@ def tile_picked_gcn_mlp_none_sub_l_kernel(tc, xT, w1, w2, gate, pos1, pos2, pos3
         def add_turned(acc, picked, d):
             nc.tensor.matmul(acc, picked, ident[:], is_transpose=True, start=(d == 0), stop=(d == D - 1))
 
-        def round_sums(copy, b, v, acc):
-            copy(zT[v][:, :, 32 * b : 32 * (b + 1), :], acc.rearrange("r (q u e) -> r u q e", u=2, e=2))
+        def round_sums(copy, first_block, blocks, v, acc):
+            copy(
+                zT[v][:, :, 32 * first_block : 32 * (first_block + blocks), :],
+                acc.rearrange("r (q u e) -> r u q e", u=2, e=2),
+            )
 
-        parts = {b: (((0, 1), 0), ((2, 3), 1)) for b in (1, 2, 3)}
+        early = [psum.tile([P, BLOCKS - 1, P], F32, name=f"early{v}") for v in range(HALVES)]
+        parts = {1: (((0, 1), 1), ((2, 3), 2)), 2: (((0, 1), 0), ((2, 3), 1)), 3: (((0, 1), 0), ((2, 3), 1))}
+        after = {1: ("xlast1", "xlast0"), 2: ("wraw1_3", "wq1_2"), 3: ("wraw2_3", "wq2_2")}
         for b in range(BLOCKS - 1):
             waiting = {}
             for k, (passes, d) in enumerate(parts[b + 1]):
-                grouped = turns.tile([P, len(passes), P, 4], BF16, name=f"turn{b}_{k}", align_bytes=64)
+                grouped = turns.tile([P, len(passes), P, 4], BF16, name=after[b + 1][k], align_bytes=64)
                 for e, c in enumerate(passes):
-                    interleave(nc.scalar.copy, grouped[:, e], b + 1, c, slice(0, P))
+                    interleave(nc.scalar.copy, grouped[:, e], wraw[b + 1][c][:])
                 waiting[d] = (k, passes, grouped)
-            bank = psum.tile([P, T], F32, name="bank")
-            acc = [psum.tile([P, P], F32, name=f"acc{v}") for v in range(HALVES)]
+            bank = psum.tile([P, T], F32, name=f"hbank{b % 2}")
             for d in range(D):
                 if d in waiting:
                     k, passes, grouped = waiting[d]
@@ -188,27 +207,30 @@ def tile_picked_gcn_mlp_none_sub_l_kernel(tc, xT, w1, w2, gate, pos1, pos2, pos3
                     for c in passes:
                         multiply(bank[:], b + 1, c, slice(0, T))
                     if passes[-1] == PASSES - 1:
+                        h[b + 1] = turns.tile([P, T], F32, name=f"h{b + 1}", align_bytes=64)
                         nc.scalar.copy(h[b + 1][:], bank[:])
-                    picked = turns.tile([P, V], F32, name=f"turn{b}_{k}", align_bytes=64)
-                else:
-                    picked = keep.tile([P, V], F32, name=f"picked{b}_{d}")
-                gather(b, d, slice(0, V), picked[:])
+                    group = turns.tile([P, D - d, V], F32, name=after[b + 1][k], align_bytes=64)
+                    start = d
+                elif d == 0:
+                    group = keep.tile([P, D, V], F32, name=f"picked{b}")
+                    start = 0
+                picked = group[:, d - start, :]
+                gather(b, d, slice(0, V), picked)
                 for v in range(HALVES):
-                    add_turned(acc[v][:], picked[:, P * v : P * (v + 1)], d)
-            for v in range(HALVES):
-                round_sums(nc.scalar.copy, b, v, acc[v][:])
-            if b == 1:
-                nc.scalar.copy(w2g[:], w2raw[:].rearrange("p t m -> p m t"))
-            if b == 2:
-                nc.vector.quantize_mx(out=w2q[:].bitcast(FP8X4), scales=w2s[:], in_=w2g[:].rearrange("p m t -> p (m t)"))
+                    add_turned(early[v][:, b, :], picked[:, P * v : P * (v + 1)], d)
+        w2g = turns.tile([P, N, 4], BF16, name="wraw3_3", align_bytes=64)
+        nc.scalar.copy(w2g[:], w2raw[:].rearrange("p t m -> p m t"))
+        nc.vector.quantize_mx(out=w2q[:].bitcast(FP8X4), scales=w2s[:], in_=w2g[:].rearrange("p m t -> p (m t)"))
+        for v in range(HALVES):
+            round_sums(nc.scalar.copy, 0, BLOCKS - 1, v, early[v][:].rearrange("r b i -> r (b i)"))
 
         b = BLOCKS - 1
-        zbank = [psum1.tile([P, 2, P], F32, name=f"zbank{v}") for v in range(HALVES)]
+        zbank = [psum.tile([P, 2, P], F32, name=f"zbank{v}") for v in range(HALVES)]
         zg = [keep.tile([P, P, 4], BF16, name=f"zg{v}", align_bytes=64) for v in range(HALVES)]
         zq = [keep.tile([P, P], U32, name=f"zq{v}", align_bytes=64) for v in range(HALVES)]
         zs = [keep.tile([P, P], U8, name=f"zs{v}", align_bytes=64) for v in range(HALVES)]
         result = [keep.tile([P, P], F32, name=f"result{v}") for v in range(HALVES)]
-        acc = [psum.tile([P, P], F32, name=f"acc{v}") for v in range(HALVES)]
+        acc = [psum.tile([P, P], F32, name=f"last{v}") for v in range(HALVES)]
 
         def pick_half(v):
             for d in range(D):
@@ -227,21 +249,21 @@ def tile_picked_gcn_mlp_none_sub_l_kernel(tc, xT, w1, w2, gate, pos1, pos2, pos3
 
         def second_layer(v, copy, queue):
             nc.vector.quantize_mx(out=zq[v][:].bitcast(FP8X4), scales=zs[v][:], in_=zg[v][:].rearrange("p r t -> p (r t)"))
-            bank = psum.tile([P, T], F32, name="bank")
+            bank = psum.tile([P, P], F32, name=f"hbank{1 - v}")
             nc.tensor.matmul_mx(
-                out=bank[:, :P],
+                out=bank[:],
                 lhsT=w2q[:].bitcast(FP8X4), lhsT_scale=w2s[:],
                 rhs=zq[v][:].bitcast(FP8X4), rhs_scale=zs[v][:],
                 start=True, stop=True,
             )
-            copy(result[v][:], bank[:, :P])
+            copy(result[v][:], bank[:])
             queue.dma_start(out=out[:, P * v : P * (v + 1)], in_=result[v][:])
 
         pick_half(0)
-        round_sums(nc.scalar.copy, b, 0, acc[0][:])
+        round_sums(nc.scalar.copy, b, 1, 0, acc[0][:])
         turn_back(0)
         pick_half(1)
         second_layer(0, nc.scalar.copy, nc.sync)
-        round_sums(nc.vector.tensor_copy, b, 1, acc[1][:])
+        round_sums(nc.vector.tensor_copy, b, 1, 1, acc[1][:])
         turn_back(1)
         second_layer(1, nc.vector.tensor_copy, nc.sync)

@@ -38,7 +38,7 @@ def tile_picked_gcn_mlp_none_sub_l_kernel(tc, xT, w1, w2, gate, pos1, pos2, pos3
         xlast = [turns.tile([P, 4, HT], F32, name=f"xlast{a}", align_bytes=64) for a in range(2)]
         wraw = [[turns.tile([P, 4, P], F32, name=f"wraw{b}_{c}", align_bytes=64) for c in range(PASSES)] for b in range(BLOCKS)]
         w2raw = keep.tile([P, 4, N], F32, name="w2raw")
-        gate_rows = keep.tile([P, V], F32, name="gate_rows")
+        gate_rows = turns.tile([P, V], F32, name="wg0", align_bytes=64)
         nc.gpsimd.memset(gate_rows[: P - D, :], 0.0)
 
         def load_w1(b, c):
@@ -50,11 +50,10 @@ def tile_picked_gcn_mlp_none_sub_l_kernel(tc, xT, w1, w2, gate, pos1, pos2, pos3
         def load_list(d):
             nc.sync.dma_start(pos[d][:], lists_in[d])
 
+        nc.sync.dma_start(out=gate_rows[P - D : P - D + 4, :], in_=gate[0:4, 0, :])
+        nc.sync.dma_start(out=gate_rows[P - 2 :, :], in_=gate[4:6, 0, :])
         for c in range(2):
             load_w1(0, c)
-            if c == 0:
-                nc.sync.dma_start(out=gate_rows[P - D : P - D + 4, :], in_=gate[0:4, 0, :])
-                nc.sync.dma_start(out=gate_rows[P - 2 :, :], in_=gate[4:6, 0, :])
         for c in range(LAST):
             nc.sync.dma_start(out=xraw[c][:], in_=xT[512 * c : 512 * (c + 1), :].rearrange("(p j) w -> p j w", j=4))
         load_w1(0, 2)
@@ -99,9 +98,10 @@ def tile_picked_gcn_mlp_none_sub_l_kernel(tc, xT, w1, w2, gate, pos1, pos2, pos3
                             ident[:],
                         )
                 pair = keep.tile([P, 2, V], F32, name=f"gates{g}")
-                (nc.vector.tensor_copy if g == 1 else nc.scalar.copy)(pair[:].rearrange("p e v -> p (e v)"), gate_bank[:])
+                if g < 2:
+                    (nc.vector.tensor_copy if g == 1 else nc.scalar.copy)(pair[:].rearrange("p e v -> p (e v)"), gate_bank[:])
                 gates.append(pair)
-            return gates
+            return gates, gate_bank
 
         def interleave(copy, grouped, raw):
             copy(grouped.rearrange("p (c i) t -> p c t i", i=4), raw.rearrange("p t (c i) -> p c t i", i=4))
@@ -149,15 +149,17 @@ def tile_picked_gcn_mlp_none_sub_l_kernel(tc, xT, w1, w2, gate, pos1, pos2, pos3
                 out=xq[c][0][:, nodes].bitcast(FP8X4), scales=xq[c][1][:, nodes], in_=grouped[:].rearrange("p w t -> p (w t)")
             )
 
-        grouped = keep.tile([P, 2, P, 4], BF16, name="wg0", align_bytes=64)
-        interleave(nc.scalar.copy, grouped[:, 0], wraw[0][0][:])
+        gates, gate_bank = spread_gates()
+        grouped = turns.tile([P, 2, P, 4], BF16, name="wg0", align_bytes=64)
+        interleave(nc.vector.tensor_copy, grouped[:, 0], wraw[0][0][:])
         interleave(nc.vector.tensor_copy, grouped[:, 1], wraw[0][1][:])
         quantise_w1(grouped[:], 0, (0, 1))
-        gates = spread_gates()
         first = [psum.tile([P, HT], F32, name=f"hbank{a}") for a in range(2)]
         halves = [slice(HT * a, HT * (a + 1)) for a in range(2)]
         for c in range(LAST):
             quantise_x(c, xraw[c], slice(0, T), 176, "xg")
+            if c == 0:
+                nc.scalar.copy(gates[2][:].rearrange("p e v -> p (e v)"), gate_bank[:])
             if c == 2:
                 grouped = turns.tile([P, 2, P, 4], BF16, name="xraw2", align_bytes=64)
                 interleave(nc.scalar.copy, grouped[:, 0], wraw[0][2][:])
@@ -171,7 +173,6 @@ def tile_picked_gcn_mlp_none_sub_l_kernel(tc, xT, w1, w2, gate, pos1, pos2, pos3
         nc.scalar.copy(h[0][:, halves[0]], first[0][:])
         nc.vector.tensor_copy(h[0][:, halves[1]], first[1][:])
 
-        w2q = keep.tile([P, N], U32, name="w2q", align_bytes=64)
         w2s = keep.tile([P, N], U8, name="w2s", align_bytes=64)
         zT = [keep.tile([P, 2, P, 2], BF16, name=f"zT{v}") for v in range(HALVES)]
 
@@ -220,7 +221,6 @@ def tile_picked_gcn_mlp_none_sub_l_kernel(tc, xT, w1, w2, gate, pos1, pos2, pos3
                     add_turned(early[v][:, b, :], picked[:, P * v : P * (v + 1)], d)
         w2g = turns.tile([P, N, 4], BF16, name="wraw3_3", align_bytes=64)
         nc.scalar.copy(w2g[:], w2raw[:].rearrange("p t m -> p m t"))
-        nc.vector.quantize_mx(out=w2q[:].bitcast(FP8X4), scales=w2s[:], in_=w2g[:].rearrange("p m t -> p (m t)"))
         for v in range(HALVES):
             round_sums(nc.scalar.copy, 0, BLOCKS - 1, v, early[v][:].rearrange("r b i -> r (b i)"))
 
@@ -232,8 +232,14 @@ def tile_picked_gcn_mlp_none_sub_l_kernel(tc, xT, w1, w2, gate, pos1, pos2, pos3
         result = [keep.tile([P, P], F32, name=f"result{v}") for v in range(HALVES)]
         acc = [psum.tile([P, P], F32, name=f"last{v}") for v in range(HALVES)]
 
+        for d in range(D - 2):
+            picked = keep.tile([P, V], F32, name=f"picked{b}_{d}")
+            gather(b, d, slice(0, V), picked[:])
+            for v in range(HALVES):
+                add_turned(acc[v][:], picked[:, P * v : P * (v + 1)], d)
+
         def pick_half(v):
-            for d in range(D):
+            for d in range(D - 2, D):
                 picked = keep.tile([P, P], F32, name=f"picked{b}_{d}_{v}")
                 gather(b, d, slice(P * v, P * (v + 1)), picked[:])
                 add_turned(acc[v][:], picked[:], d)
@@ -263,6 +269,8 @@ def tile_picked_gcn_mlp_none_sub_l_kernel(tc, xT, w1, w2, gate, pos1, pos2, pos3
         round_sums(nc.scalar.copy, b, 1, 0, acc[0][:])
         turn_back(0)
         pick_half(1)
+        w2q = turns.tile([P, N], U32, name="h3", align_bytes=64)
+        nc.vector.quantize_mx(out=w2q[:].bitcast(FP8X4), scales=w2s[:], in_=w2g[:].rearrange("p m t -> p (m t)"))
         second_layer(0, nc.scalar.copy, nc.sync)
         round_sums(nc.vector.tensor_copy, b, 1, 1, acc[1][:])
         turn_back(1)

@@ -191,26 +191,31 @@ def tile_picked_gcn_mlp_none_sub_l_kernel(tc, xT, w1, w2, gate, pos1, pos2, pos3
             )
 
         early = [psum.tile([P, BLOCKS - 1, P], F32, name=f"early{v}") for v in range(HALVES)]
-        parts = {1: (((0, 1), 1), ((2, 3), 2)), 2: (((0, 1), 0), ((2, 3), 1)), 3: (((0, 1), 0), ((2, 3), 1))}
-        after = {1: ("xlast1", "xlast0"), 2: ("wraw1_3", "wq1_2"), 3: ("wraw2_3", "wq2_2")}
+        ahead = {
+            (0, 1): (1, (0, 1), "xlast1"),
+            (0, 2): (1, (2, 3), "xlast0"),
+            (0, 4): (2, (0, 1), "wraw1_3"),
+            (1, 1): (2, (2, 3), "wq1_2"),
+            (1, 4): (3, (0, 1), "wraw2_3"),
+            (2, 1): (3, (2, 3), "wq2_2"),
+        }
+        banks = {}
         for b in range(BLOCKS - 1):
-            waiting = {}
-            for k, (passes, d) in enumerate(parts[b + 1]):
-                grouped = turns.tile([P, len(passes), P, 4], BF16, name=after[b + 1][k], align_bytes=64)
-                for e, c in enumerate(passes):
-                    interleave(nc.scalar.copy, grouped[:, e], wraw[b + 1][c][:])
-                waiting[d] = (k, passes, grouped)
-            bank = psum.tile([P, T], F32, name=f"hbank{b % 2}")
             for d in range(D):
-                if d in waiting:
-                    k, passes, grouped = waiting[d]
-                    quantise_w1(grouped[:], b + 1, passes)
+                if (b, d) in ahead:
+                    nb, passes, name = ahead[b, d]
+                    grouped = turns.tile([P, len(passes), P, 4], BF16, name=name, align_bytes=64)
+                    for e, c in enumerate(passes):
+                        interleave(nc.scalar.copy, grouped[:, e], wraw[nb][c][:])
+                    quantise_w1(grouped[:], nb, passes)
+                    if passes[0] == 0:
+                        banks[nb] = psum.tile([P, T], F32, name=f"hbank{nb % 2}")
                     for c in passes:
-                        multiply(bank[:], b + 1, c, slice(0, T))
+                        multiply(banks[nb][:], nb, c, slice(0, T))
                     if passes[-1] == PASSES - 1:
-                        h[b + 1] = turns.tile([P, T], F32, name=f"h{b + 1}", align_bytes=64)
-                        nc.scalar.copy(h[b + 1][:], bank[:])
-                    group = turns.tile([P, D - d, V], F32, name=after[b + 1][k], align_bytes=64)
+                        h[nb] = turns.tile([P, T], F32, name=f"h{nb}", align_bytes=64)
+                        nc.scalar.copy(h[nb][:], banks[nb][:])
+                    group = turns.tile([P, D - d, V], F32, name=name, align_bytes=64)
                     start = d
                 elif d == 0:
                     group = keep.tile([P, D, V], F32, name=f"picked{b}")
@@ -255,7 +260,7 @@ def tile_picked_gcn_mlp_none_sub_l_kernel(tc, xT, w1, w2, gate, pos1, pos2, pos3
 
         def second_layer(v, copy, queue):
             nc.vector.quantize_mx(out=zq[v][:].bitcast(FP8X4), scales=zs[v][:], in_=zg[v][:].rearrange("p r t -> p (r t)"))
-            bank = psum.tile([P, P], F32, name=f"hbank{1 - v}")
+            bank = psum.tile([P, P], F32, name=f"hbank{v}")
             nc.tensor.matmul_mx(
                 out=bank[:],
                 lhsT=w2q[:].bitcast(FP8X4), lhsT_scale=w2s[:],

@@ -38,7 +38,7 @@ def tile_picked_gcn_mlp_none_sub_l_kernel(tc, xT, w1, w2, gate, pos1, pos2, pos3
         xlast = [turns.tile([P, 4, HT], F32, name=f"xlast{a}", align_bytes=64) for a in range(2)]
         wraw = [[turns.tile([P, 4, P], F32, name=f"wraw{b}_{c}", align_bytes=64) for c in range(PASSES)] for b in range(BLOCKS)]
         w2raw = keep.tile([P, 4, N], F32, name="w2raw")
-        gate_rows = turns.tile([P, V], F32, name="wg0", align_bytes=64)
+        gate_rows = turns.tile([P, V], F32, name="xg", align_bytes=64)
         nc.gpsimd.memset(gate_rows[: P - D, :], 0.0)
 
         def load_w1(b, c):
@@ -50,10 +50,10 @@ def tile_picked_gcn_mlp_none_sub_l_kernel(tc, xT, w1, w2, gate, pos1, pos2, pos3
         def load_list(d):
             nc.sync.dma_start(pos[d][:], lists_in[d])
 
+        load_w1(0, 0)
         nc.sync.dma_start(out=gate_rows[P - D : P - D + 4, :], in_=gate[0:4, 0, :])
         nc.sync.dma_start(out=gate_rows[P - 2 :, :], in_=gate[4:6, 0, :])
-        for c in range(2):
-            load_w1(0, c)
+        load_w1(0, 1)
         for c in range(LAST):
             nc.sync.dma_start(out=xraw[c][:], in_=xT[512 * c : 512 * (c + 1), :].rearrange("(p j) w -> p j w", j=4))
         load_w1(0, 2)
@@ -84,9 +84,9 @@ def tile_picked_gcn_mlp_none_sub_l_kernel(tc, xT, w1, w2, gate, pos1, pos2, pos3
             gate_bank = psum.tile([P, T], F32, name="zbank0")
             for v in range(HALVES):
                 nc.tensor.transpose(gate_bank[:, P * v : P * (v + 1)], gate_rows[:, P * v : P * (v + 1)], ident[:])
-            gate_cols = turns.tile([P, HALVES, 8], F32, name="xg", align_bytes=64)
-            nc.vector.tensor_copy(gate_cols[:], gate_bank[:, :V].rearrange("p (v r) -> p v r", v=HALVES)[:, :, P - 8 :])
-            gates = []
+            gate_cols = keep.tile([P, HALVES, 8], F32, name="gate_cols")
+            nc.scalar.copy(gate_cols[:], gate_bank[:, :V].rearrange("p (v r) -> p v r", v=HALVES)[:, :, P - 8 :])
+            banks = []
             for g in range(D // 2):
                 gate_bank = psum.tile([P, T], F32, name=("zbank1", "last0", "last1")[g])
                 for e in range(2):
@@ -97,11 +97,15 @@ def tile_picked_gcn_mlp_none_sub_l_kernel(tc, xT, w1, w2, gate, pos1, pos2, pos3
                             gate_cols[:, v, 2 + d : 3 + d].to_broadcast([P, P]),
                             ident[:],
                         )
-                pair = keep.tile([P, 2, V], F32, name=f"gates{g}")
-                if g < 2:
-                    (nc.vector.tensor_copy if g == 1 else nc.scalar.copy)(pair[:].rearrange("p e v -> p (e v)"), gate_bank[:])
-                gates.append(pair)
-            return gates, gate_bank
+                banks.append(gate_bank)
+            return banks
+
+        gates = []
+
+        def keep_gates(bank, name):
+            pair = turns.tile([P, 2, V], F32, name=name, align_bytes=64)
+            nc.scalar.copy(pair[:].rearrange("p e v -> p (e v)"), bank[:])
+            gates.append(pair)
 
         def interleave(copy, grouped, raw):
             copy(grouped.rearrange("p (c i) t -> p c t i", i=4), raw.rearrange("p t (c i) -> p c t i", i=4))
@@ -149,8 +153,9 @@ def tile_picked_gcn_mlp_none_sub_l_kernel(tc, xT, w1, w2, gate, pos1, pos2, pos3
                 out=xq[c][0][:, nodes].bitcast(FP8X4), scales=xq[c][1][:, nodes], in_=grouped[:].rearrange("p w t -> p (w t)")
             )
 
-        gates, gate_bank = spread_gates()
-        grouped = turns.tile([P, 2, P, 4], BF16, name="wg0", align_bytes=64)
+        gate_banks = spread_gates()
+        keep_gates(gate_banks[0], "gates0")
+        grouped = turns.tile([P, 2, P, 4], BF16, name="xg", align_bytes=64)
         interleave(nc.vector.tensor_copy, grouped[:, 0], wraw[0][0][:])
         interleave(nc.vector.tensor_copy, grouped[:, 1], wraw[0][1][:])
         quantise_w1(grouped[:], 0, (0, 1))
@@ -158,8 +163,8 @@ def tile_picked_gcn_mlp_none_sub_l_kernel(tc, xT, w1, w2, gate, pos1, pos2, pos3
         halves = [slice(HT * a, HT * (a + 1)) for a in range(2)]
         for c in range(LAST):
             quantise_x(c, xraw[c], slice(0, T), 176, "xg")
-            if c == 0:
-                nc.scalar.copy(gates[2][:].rearrange("p e v -> p (e v)"), gate_bank[:])
+            if c < 2:
+                keep_gates(gate_banks[c + 1], f"xraw{c}")
             if c == 2:
                 grouped = turns.tile([P, 2, P, 4], BF16, name="xraw2", align_bytes=64)
                 interleave(nc.scalar.copy, grouped[:, 0], wraw[0][2][:])
@@ -195,9 +200,9 @@ def tile_picked_gcn_mlp_none_sub_l_kernel(tc, xT, w1, w2, gate, pos1, pos2, pos3
             (0, 1): (1, (0, 1), "xlast1"),
             (0, 2): (1, (2, 3), "xlast0"),
             (0, 4): (2, (0, 1), "wraw1_3"),
-            (1, 1): (2, (2, 3), "wq1_2"),
+            (1, 2): (2, (2, 3), "wq1_2"),
             (1, 4): (3, (0, 1), "wraw2_3"),
-            (2, 1): (3, (2, 3), "wq2_2"),
+            (2, 2): (3, (2, 3), "wq2_2"),
         }
         banks = {}
         for b in range(BLOCKS - 1):

@@ -6,10 +6,18 @@ from concourse.masks import make_identity
 K, T, D, V, H, N = 2048, 512, 6, 256, 512, 128
 P = 128
 PASSES = K // 512
+LAST = PASSES - 1
 BLOCKS = H // P
 HALVES = V // P
+HT = T // 2
 FLOPS = 2 * K * H * T + 2 * H * N * V
 BYTES = 4 * (K * T + K * H + H * N + D * V + N * V) + 2 * D * P * (V // 16)
+
+SCALAR_COLUMNS_WHOLE = 176
+SCALAR_COLUMNS_LAST = (128, 80)
+FINISH_AT = 2
+BEGIN_AT = 4
+SPLIT_LISTS = 2
 
 F32 = mybir.dt.float32
 BF16 = mybir.dt.bfloat16
@@ -32,8 +40,6 @@ def tile_picked_gcn_mlp_none_sub_l_kernel(tc, xT, w1, w2, gate, pos1, pos2, pos3
 
         pos = [lists.tile([P, V // 16], U16, name=f"pos{d}") for d in range(D)]
 
-        LAST = PASSES - 1
-        HT = T // 2
         xraw = [turns.tile([P, 4, T], F32, name=f"xraw{c}", align_bytes=64) for c in range(LAST)]
         xlast = [turns.tile([P, 4, HT], F32, name=f"xlast{a}", align_bytes=64) for a in range(2)]
         wraw = [[turns.tile([P, 4, P], F32, name=f"wraw{b}_{c}", align_bytes=64) for c in range(PASSES)] for b in range(BLOCKS)]
@@ -51,8 +57,8 @@ def tile_picked_gcn_mlp_none_sub_l_kernel(tc, xT, w1, w2, gate, pos1, pos2, pos3
             nc.sync.dma_start(pos[d][:], lists_in[d])
 
         load_w1(0, 0)
-        nc.sync.dma_start(out=gate_rows[P - D : P - D + 4, :], in_=gate[0:4, 0, :])
-        nc.sync.dma_start(out=gate_rows[P - 2 :, :], in_=gate[4:6, 0, :])
+        nc.sync.dma_start(out=gate_rows[P - D : P - 2, :], in_=gate[0 : D - 2, 0, :])
+        nc.sync.dma_start(out=gate_rows[P - 2 :, :], in_=gate[D - 2 : D, 0, :])
         load_w1(0, 1)
         for c in range(LAST):
             nc.sync.dma_start(out=xraw[c][:], in_=xT[512 * c : 512 * (c + 1), :].rearrange("(p j) w -> p j w", j=4))
@@ -72,7 +78,7 @@ def tile_picked_gcn_mlp_none_sub_l_kernel(tc, xT, w1, w2, gate, pos1, pos2, pos3
         load_list(4)
         load_list(5)
         load_w1(1, 3)
-        for b in (2, 3):
+        for b in range(2, BLOCKS):
             for c in range(PASSES):
                 load_w1(b, c)
         nc.sync.dma_start(out=w2raw[:], in_=w2.rearrange("(p j) m -> p j m", j=4))
@@ -80,50 +86,35 @@ def tile_picked_gcn_mlp_none_sub_l_kernel(tc, xT, w1, w2, gate, pos1, pos2, pos3
         ident = keep.tile([P, P], F32, name="ident")
         make_identity(nc, ident[:])
 
-        def spread_gates():
-            gate_bank = psum.tile([P, T], F32, name="zbank0")
-            for v in range(HALVES):
-                nc.tensor.transpose(gate_bank[:, P * v : P * (v + 1)], gate_rows[:, P * v : P * (v + 1)], ident[:])
-            gate_cols = keep.tile([P, HALVES, 8], F32, name="gate_cols")
-            nc.scalar.copy(gate_cols[:], gate_bank[:, :V].rearrange("p (v r) -> p v r", v=HALVES)[:, :, P - 8 :])
-            banks = []
-            for g in range(D // 2):
-                gate_bank = psum.tile([P, T], F32, name=("zbank1", "last0", "last1")[g])
-                for e in range(2):
-                    for v in range(HALVES):
-                        d = 2 * g + e
-                        nc.tensor.transpose(
-                            gate_bank[:, (2 * e + v) * P : (2 * e + v + 1) * P],
-                            gate_cols[:, v, 2 + d : 3 + d].to_broadcast([P, P]),
-                            ident[:],
-                        )
-                banks.append(gate_bank)
-            return banks
+        cols_bank = psum.tile([P, T], F32, name="zbank0")
+        for v in range(HALVES):
+            nc.tensor.transpose(cols_bank[:, P * v : P * (v + 1)], gate_rows[:, P * v : P * (v + 1)], ident[:])
+        gate_cols = keep.tile([P, HALVES, D], F32, name="gate_cols")
+        nc.scalar.copy(gate_cols[:], cols_bank[:, :V].rearrange("p (v r) -> p v r", v=HALVES)[:, :, P - D :])
+        gate_banks = []
+        for g, name in enumerate(("zbank1", "last0", "last1")):
+            pair_bank = psum.tile([P, T], F32, name=name)
+            for e in range(2):
+                for v in range(HALVES):
+                    d = 2 * g + e
+                    nc.tensor.transpose(
+                        pair_bank[:, (2 * e + v) * P : (2 * e + v + 1) * P],
+                        gate_cols[:, v, d : d + 1].to_broadcast([P, P]),
+                        ident[:],
+                    )
+            gate_banks.append(pair_bank)
 
         gates = []
 
-        def keep_gates(bank, name):
+        def keep_gates(g, name):
             pair = turns.tile([P, 2, V], F32, name=name, align_bytes=64)
-            nc.scalar.copy(pair[:].rearrange("p e v -> p (e v)"), bank[:])
+            nc.scalar.copy(pair[:].rearrange("p e v -> p (e v)"), gate_banks[g][:])
             gates.append(pair)
 
         def interleave(copy, grouped, raw):
             copy(grouped.rearrange("p (c i) t -> p c t i", i=4), raw.rearrange("p t (c i) -> p c t i", i=4))
 
         wq = {}
-
-        def quantise_w1(grouped, b, passes):
-            n = len(passes)
-            codes = turns.tile([P, n, P], U32, name=f"wq{b}_{passes[0]}", align_bytes=64)
-            scales = keep.tile([P, n, P], U8, name=f"ws{b}_{passes[0]}", align_bytes=64)
-            nc.vector.quantize_mx(
-                out=codes[:].rearrange("p c w -> p (c w)").bitcast(FP8X4),
-                scales=scales[:].rearrange("p c w -> p (c w)"),
-                in_=grouped.rearrange("p c w t -> p (c w t)"),
-            )
-            for e, c in enumerate(passes):
-                wq[b, c] = (codes[:, e, :], scales[:, e, :])
-
         xq = [
             (
                 keep.tile([P, T], U32, name=f"xq{c}", align_bytes=64),
@@ -133,6 +124,25 @@ def tile_picked_gcn_mlp_none_sub_l_kernel(tc, xT, w1, w2, gate, pos1, pos2, pos3
         ]
         h = {0: keep.tile([P, T], F32, name="h0")}
 
+        def quantise_w1(grouped, b, first_pass):
+            codes = turns.tile([P, 2, P], U32, name=f"wq{b}_{first_pass}", align_bytes=64)
+            scales = keep.tile([P, 2, P], U8, name=f"ws{b}_{first_pass}", align_bytes=64)
+            nc.vector.quantize_mx(
+                out=codes[:].rearrange("p c w -> p (c w)").bitcast(FP8X4),
+                scales=scales[:].rearrange("p c w -> p (c w)"),
+                in_=grouped[:].rearrange("p c w t -> p (c w t)"),
+            )
+            for e in range(2):
+                wq[b, first_pass + e] = (codes[:, e, :], scales[:, e, :])
+
+        def quantise_x(c, raw, nodes, cut, name):
+            grouped = turns.tile([P, nodes.stop - nodes.start, 4], BF16, name=name, align_bytes=64)
+            interleave(nc.scalar.copy, grouped[:, :cut, :], raw[:, :, :cut])
+            interleave(nc.vector.tensor_copy, grouped[:, cut:, :], raw[:, :, cut:])
+            nc.vector.quantize_mx(
+                out=xq[c][0][:, nodes].bitcast(FP8X4), scales=xq[c][1][:, nodes], in_=grouped[:].rearrange("p w t -> p (w t)")
+            )
+
         def multiply(bank, b, c, nodes):
             nc.tensor.matmul_mx(
                 out=bank,
@@ -141,42 +151,34 @@ def tile_picked_gcn_mlp_none_sub_l_kernel(tc, xT, w1, w2, gate, pos1, pos2, pos3
                 rhs=xq[c][0][:, nodes].bitcast(FP8X4),
                 rhs_scale=xq[c][1][:, nodes],
                 start=(c == 0),
-                stop=(c == PASSES - 1),
+                stop=(c == LAST),
             )
 
-        def quantise_x(c, raw, nodes, cut, name):
-            width = nodes.stop - nodes.start
-            grouped = turns.tile([P, width, 4], BF16, name=name, align_bytes=64)
-            interleave(nc.scalar.copy, grouped[:, :cut, :], raw[:, :, :cut])
-            interleave(nc.vector.tensor_copy, grouped[:, cut:, :], raw[:, :, cut:])
-            nc.vector.quantize_mx(
-                out=xq[c][0][:, nodes].bitcast(FP8X4), scales=xq[c][1][:, nodes], in_=grouped[:].rearrange("p w t -> p (w t)")
-            )
-
-        gate_banks = spread_gates()
-        keep_gates(gate_banks[0], "gates0")
+        keep_gates(0, "gates0")
         grouped = turns.tile([P, 2, P, 4], BF16, name="xg", align_bytes=64)
-        interleave(nc.vector.tensor_copy, grouped[:, 0], wraw[0][0][:])
-        interleave(nc.vector.tensor_copy, grouped[:, 1], wraw[0][1][:])
-        quantise_w1(grouped[:], 0, (0, 1))
-        first = [psum.tile([P, HT], F32, name=f"hbank{a}") for a in range(2)]
-        halves = [slice(HT * a, HT * (a + 1)) for a in range(2)]
+        for c in range(2):
+            interleave(nc.vector.tensor_copy, grouped[:, c], wraw[0][c][:])
+        quantise_w1(grouped, 0, 0)
+        pieces = [slice(0, HT), slice(HT, HT + P), slice(HT + P, T)]
+        first_banks = [psum.tile([P, s.stop - s.start], F32, name=n) for s, n in zip(pieces, ("hbank0", "hbank1", "zbank0"))]
         for c in range(LAST):
-            quantise_x(c, xraw[c], slice(0, T), 176, "xg")
-            if c < 2:
-                keep_gates(gate_banks[c + 1], f"xraw{c}")
-            if c == 2:
-                grouped = turns.tile([P, 2, P, 4], BF16, name="xraw2", align_bytes=64)
+            quantise_x(c, xraw[c], slice(0, T), SCALAR_COLUMNS_WHOLE, "xg")
+            if c + 1 < len(gate_banks):
+                keep_gates(c + 1, f"xraw{c}")
+            else:
+                grouped = turns.tile([P, 2, P, 4], BF16, name=f"xraw{c}", align_bytes=64)
                 interleave(nc.scalar.copy, grouped[:, 0], wraw[0][2][:])
                 interleave(nc.vector.tensor_copy, grouped[:, 1], wraw[0][3][:])
-                quantise_w1(grouped[:], 0, (2, 3))
-            for a in range(2):
-                multiply(first[a][:], 0, c, halves[a])
-        for a in range(2):
-            quantise_x(LAST, xlast[a], halves[a], (128, 80)[a], ("xg", "xlast0")[a])
-            multiply(first[a][:], 0, LAST, halves[a])
-        nc.scalar.copy(h[0][:, halves[0]], first[0][:])
-        nc.vector.tensor_copy(h[0][:, halves[1]], first[1][:])
+                quantise_w1(grouped, 0, 2)
+            for bank, nodes in zip(first_banks, pieces):
+                multiply(bank[:], 0, c, nodes)
+        quantise_x(LAST, xlast[0], slice(0, HT), SCALAR_COLUMNS_LAST[0], "xg")
+        multiply(first_banks[0][:], 0, LAST, pieces[0])
+        quantise_x(LAST, xlast[1], slice(HT, T), SCALAR_COLUMNS_LAST[1], "xlast0")
+        for bank, nodes in zip(first_banks[1:], pieces[1:]):
+            multiply(bank[:], 0, LAST, nodes)
+        for copy, bank, nodes in zip((nc.scalar.copy, nc.scalar.copy, nc.vector.tensor_copy), first_banks, pieces):
+            copy(h[0][:, nodes], bank[:])
 
         w2s = keep.tile([P, N], U8, name="w2s", align_bytes=64)
         zT = [keep.tile([P, 2, P, 2], BF16, name=f"zT{v}") for v in range(HALVES)]
@@ -196,63 +198,59 @@ def tile_picked_gcn_mlp_none_sub_l_kernel(tc, xT, w1, w2, gate, pos1, pos2, pos3
             )
 
         early = [psum.tile([P, BLOCKS - 1, P], F32, name=f"early{v}") for v in range(HALVES)]
-        ahead = {
-            (0, 1): (1, (0, 1), "xlast1"),
-            (0, 2): (1, (2, 3), "xlast0"),
-            (0, 4): (2, (0, 1), "wraw1_3"),
-            (1, 2): (2, (2, 3), "wq1_2"),
-            (1, 4): (3, (0, 1), "wraw2_3"),
-            (2, 2): (3, (2, 3), "wq2_2"),
-        }
-        banks = {}
+        ahead = {(0, 1): (1, 0, "xlast1"), (0, FINISH_AT): (1, 2, "xlast0")}
+        for b in range(2, BLOCKS):
+            ahead[b - 2, BEGIN_AT] = (b, 0, f"wraw{b - 1}_{LAST}")
+            ahead[b - 1, FINISH_AT] = (b, 2, f"wq{b - 1}_2")
+        hbanks = {}
         for b in range(BLOCKS - 1):
             for d in range(D):
                 if (b, d) in ahead:
-                    nb, passes, name = ahead[b, d]
-                    grouped = turns.tile([P, len(passes), P, 4], BF16, name=name, align_bytes=64)
-                    for e, c in enumerate(passes):
-                        interleave(nc.scalar.copy, grouped[:, e], wraw[nb][c][:])
-                    quantise_w1(grouped[:], nb, passes)
-                    if passes[0] == 0:
-                        banks[nb] = psum.tile([P, T], F32, name=f"hbank{nb % 2}")
-                    for c in passes:
-                        multiply(banks[nb][:], nb, c, slice(0, T))
-                    if passes[-1] == PASSES - 1:
-                        h[nb] = turns.tile([P, T], F32, name=f"h{nb}", align_bytes=64)
-                        nc.scalar.copy(h[nb][:], banks[nb][:])
-                    group = turns.tile([P, D - d, V], F32, name=name, align_bytes=64)
-                    start = d
+                    coming, first_pass, name = ahead[b, d]
+                    grouped = turns.tile([P, 2, P, 4], BF16, name=name, align_bytes=64)
+                    for e in range(2):
+                        interleave(nc.scalar.copy, grouped[:, e], wraw[coming][first_pass + e][:])
+                    quantise_w1(grouped, coming, first_pass)
+                    if first_pass == 0:
+                        hbanks[coming] = psum.tile([P, T], F32, name=f"hbank{coming % 2}")
+                    for e in range(2):
+                        multiply(hbanks[coming][:], coming, first_pass + e, slice(0, T))
+                    if first_pass + 1 == LAST:
+                        h[coming] = turns.tile([P, T], F32, name=f"h{coming}", align_bytes=64)
+                        nc.scalar.copy(h[coming][:], hbanks[coming][:])
+                    terms = turns.tile([P, D - d, V], F32, name=name, align_bytes=64)
+                    first_term = d
                 elif d == 0:
-                    group = keep.tile([P, D, V], F32, name=f"picked{b}")
-                    start = 0
-                picked = group[:, d - start, :]
+                    terms = keep.tile([P, D, V], F32, name=f"terms{b}")
+                    first_term = 0
+                picked = terms[:, d - first_term, :]
                 gather(b, d, slice(0, V), picked)
                 for v in range(HALVES):
                     add_turned(early[v][:, b, :], picked[:, P * v : P * (v + 1)], d)
-        w2g = turns.tile([P, N, 4], BF16, name="wraw3_3", align_bytes=64)
+        w2g = turns.tile([P, N, 4], BF16, name=f"wraw{BLOCKS - 1}_{LAST}", align_bytes=64)
         nc.scalar.copy(w2g[:], w2raw[:].rearrange("p t m -> p m t"))
         for v in range(HALVES):
             round_sums(nc.scalar.copy, 0, BLOCKS - 1, v, early[v][:].rearrange("r b i -> r (b i)"))
 
-        b = BLOCKS - 1
+        last = BLOCKS - 1
         zbank = [psum.tile([P, 2, P], F32, name=f"zbank{v}") for v in range(HALVES)]
         zg = [keep.tile([P, P, 4], BF16, name=f"zg{v}", align_bytes=64) for v in range(HALVES)]
         zq = [keep.tile([P, P], U32, name=f"zq{v}", align_bytes=64) for v in range(HALVES)]
         zs = [keep.tile([P, P], U8, name=f"zs{v}", align_bytes=64) for v in range(HALVES)]
         result = [keep.tile([P, P], F32, name=f"result{v}") for v in range(HALVES)]
-        acc = [psum.tile([P, P], F32, name=f"last{v}") for v in range(HALVES)]
+        last_sums = [psum.tile([P, P], F32, name=f"last{v}") for v in range(HALVES)]
 
-        for d in range(D - 2):
-            picked = keep.tile([P, V], F32, name=f"picked{b}_{d}")
-            gather(b, d, slice(0, V), picked[:])
+        for d in range(D - SPLIT_LISTS):
+            whole = keep.tile([P, V], F32, name=f"whole{d}")
+            gather(last, d, slice(0, V), whole[:])
             for v in range(HALVES):
-                add_turned(acc[v][:], picked[:, P * v : P * (v + 1)], d)
+                add_turned(last_sums[v][:], whole[:, P * v : P * (v + 1)], d)
 
-        def pick_half(v):
-            for d in range(D - 2, D):
-                picked = keep.tile([P, P], F32, name=f"picked{b}_{d}_{v}")
-                gather(b, d, slice(P * v, P * (v + 1)), picked[:])
-                add_turned(acc[v][:], picked[:], d)
+        def gather_half(v):
+            for d in range(D - SPLIT_LISTS, D):
+                half = keep.tile([P, P], F32, name=f"half{d}_{v}")
+                gather(last, d, slice(P * v, P * (v + 1)), half[:])
+                add_turned(last_sums[v][:], half[:], d)
 
         def turn_back(v):
             words = zT[v][:].rearrange("r u p e -> r (u p e)").bitcast(F32)
@@ -263,25 +261,28 @@ def tile_picked_gcn_mlp_none_sub_l_kernel(tc, xT, w1, w2, gate, pos1, pos2, pos3
                 zbank[v][:].rearrange("p u r -> p r u"),
             )
 
-        def second_layer(v, copy, queue):
+        def second_layer(v, copy):
             nc.vector.quantize_mx(out=zq[v][:].bitcast(FP8X4), scales=zs[v][:], in_=zg[v][:].rearrange("p r t -> p (r t)"))
             bank = psum.tile([P, P], F32, name=f"hbank{v}")
             nc.tensor.matmul_mx(
                 out=bank[:],
-                lhsT=w2q[:].bitcast(FP8X4), lhsT_scale=w2s[:],
-                rhs=zq[v][:].bitcast(FP8X4), rhs_scale=zs[v][:],
-                start=True, stop=True,
+                lhsT=w2q[:].bitcast(FP8X4),
+                lhsT_scale=w2s[:],
+                rhs=zq[v][:].bitcast(FP8X4),
+                rhs_scale=zs[v][:],
+                start=True,
+                stop=True,
             )
             copy(result[v][:], bank[:])
-            queue.dma_start(out=out[:, P * v : P * (v + 1)], in_=result[v][:])
+            nc.sync.dma_start(out=out[:, P * v : P * (v + 1)], in_=result[v][:])
 
-        pick_half(0)
-        round_sums(nc.scalar.copy, b, 1, 0, acc[0][:])
+        gather_half(0)
+        round_sums(nc.scalar.copy, last, 1, 0, last_sums[0][:])
         turn_back(0)
-        pick_half(1)
-        w2q = turns.tile([P, N], U32, name="h3", align_bytes=64)
+        gather_half(1)
+        w2q = turns.tile([P, N], U32, name=f"h{last}", align_bytes=64)
         nc.vector.quantize_mx(out=w2q[:].bitcast(FP8X4), scales=w2s[:], in_=w2g[:].rearrange("p m t -> p (m t)"))
-        second_layer(0, nc.scalar.copy, nc.sync)
-        round_sums(nc.vector.tensor_copy, b, 1, 1, acc[1][:])
+        second_layer(0, nc.scalar.copy)
+        round_sums(nc.vector.tensor_copy, last, 1, 1, last_sums[1][:])
         turn_back(1)
-        second_layer(1, nc.vector.tensor_copy, nc.sync)
+        second_layer(1, nc.vector.tensor_copy)

@@ -68,19 +68,17 @@ def tile_picked_gcn_mlp_none_sub_l_kernel(tc, xT, w1, w2, gate, pos1, pos2, pos3
             nc.sync.dma_start(
                 out=xlast[a][:], in_=xT[512 * LAST :, HT * a : HT * (a + 1)].rearrange("(p j) w -> p j w", j=4)
             )
-        load_list(0)
-        load_list(1)
         load_w1(1, 0)
-        load_list(2)
         load_w1(1, 1)
-        load_list(3)
+        load_list(0)
         load_w1(1, 2)
-        load_list(4)
-        load_list(5)
+        load_list(1)
         load_w1(1, 3)
-        for b in range(2, BLOCKS):
-            for c in range(PASSES):
-                load_w1(b, c)
+        for c in range(PASSES):
+            load_w1(2, c)
+            load_list(2 + c)
+        for c in range(PASSES):
+            load_w1(3, c)
         nc.sync.dma_start(out=w2raw[:], in_=w2.rearrange("(p j) m -> p j m", j=4))
 
         ident = keep.tile([P, P], F32, name="ident")
@@ -122,17 +120,18 @@ def tile_picked_gcn_mlp_none_sub_l_kernel(tc, xT, w1, w2, gate, pos1, pos2, pos3
             )
             for c in range(PASSES)
         ]
-        h = {0: keep.tile([P, T], F32, name="h0")}
+        h = {}
 
-        def quantise_w1(grouped, b, first_pass):
-            codes = turns.tile([P, 2, P], U32, name=f"wq{b}_{first_pass}", align_bytes=64)
-            scales = keep.tile([P, 2, P], U8, name=f"ws{b}_{first_pass}", align_bytes=64)
+        def quantise_w1(grouped, b, first_pass, name=None):
+            count = grouped.shape[1]
+            codes = turns.tile([P, count, P], U32, name=name or f"wq{b}_{first_pass}", align_bytes=64)
+            scales = turns.tile([P, count, P], U8, name=f"ws{b}_{first_pass}", align_bytes=64)
             nc.vector.quantize_mx(
                 out=codes[:].rearrange("p c w -> p (c w)").bitcast(FP8X4),
                 scales=scales[:].rearrange("p c w -> p (c w)"),
                 in_=grouped[:].rearrange("p c w t -> p (c w t)"),
             )
-            for e in range(2):
+            for e in range(count):
                 wq[b, first_pass + e] = (codes[:, e, :], scales[:, e, :])
 
         def quantise_x(c, raw, nodes, cut, name):
@@ -177,6 +176,10 @@ def tile_picked_gcn_mlp_none_sub_l_kernel(tc, xT, w1, w2, gate, pos1, pos2, pos3
         quantise_x(LAST, xlast[1], slice(HT, T), SCALAR_COLUMNS_LAST[1], "xlast0")
         for bank, nodes in zip(first_banks[1:], pieces[1:]):
             multiply(bank[:], 0, LAST, nodes)
+        grouped1 = turns.tile([P, 2, P, 4], BF16, name="xlast1", align_bytes=64)
+        interleave(nc.vector.tensor_copy, grouped1[:, 0], wraw[1][0][:])
+        interleave(nc.vector.tensor_copy, grouped1[:, 1], wraw[1][1][:])
+        h[0] = turns.tile([P, T], F32, name="h0", align_bytes=64)
         for copy, bank, nodes in zip((nc.scalar.copy, nc.scalar.copy, nc.vector.tensor_copy), first_banks, pieces):
             copy(h[0][:, nodes], bank[:])
 
@@ -198,36 +201,47 @@ def tile_picked_gcn_mlp_none_sub_l_kernel(tc, xT, w1, w2, gate, pos1, pos2, pos3
             )
 
         early = [psum.tile([P, BLOCKS - 1, P], F32, name=f"early{v}") for v in range(HALVES)]
-        ahead = {(0, 1): (1, 0, "xlast1"), (0, FINISH_AT): (1, 2, "xlast0")}
-        for b in range(2, BLOCKS):
-            ahead[b - 2, BEGIN_AT] = (b, 0, f"wraw{b - 1}_{LAST}")
-            ahead[b - 1, FINISH_AT] = (b, 2, f"wq{b - 1}_2")
         hbanks = {}
-        for b in range(BLOCKS - 1):
-            for d in range(D):
-                if (b, d) in ahead:
-                    coming, first_pass, name = ahead[b, d]
-                    grouped = turns.tile([P, 2, P, 4], BF16, name=name, align_bytes=64)
-                    for e in range(2):
-                        interleave(nc.scalar.copy, grouped[:, e], wraw[coming][first_pass + e][:])
-                    quantise_w1(grouped, coming, first_pass)
-                    if first_pass == 0:
-                        hbanks[coming] = psum.tile([P, T], F32, name=f"hbank{coming % 2}")
-                    for e in range(2):
-                        multiply(hbanks[coming][:], coming, first_pass + e, slice(0, T))
-                    if first_pass + 1 == LAST:
-                        h[coming] = turns.tile([P, T], F32, name=f"h{coming}", align_bytes=64)
-                        nc.scalar.copy(h[coming][:], hbanks[coming][:])
-                    terms = turns.tile([P, D - d, V], F32, name=name, align_bytes=64)
-                    first_term = d
-                elif d == 0:
-                    terms = keep.tile([P, D, V], F32, name=f"terms{b}")
-                    first_term = 0
-                picked = terms[:, d - first_term, :]
+
+        def prepare(coming, first_pass, count, name):
+            grouped = turns.tile([P, count, P, 4], BF16, name=name, align_bytes=64)
+            for e in range(count):
+                interleave(nc.scalar.copy, grouped[:, e], wraw[coming][first_pass + e][:])
+            return grouped
+
+        def project(grouped, coming, first_pass, name=None):
+            quantise_w1(grouped, coming, first_pass, name)
+            if first_pass == 0:
+                hbanks[coming] = psum.tile([P, T], F32, name=f"hbank{(coming + 1) % 2}")
+            for e in range(grouped.shape[1]):
+                multiply(hbanks[coming][:], coming, first_pass + e, slice(0, T))
+
+        def keep_h(b, name):
+            h[b] = turns.tile([P, T], F32, name=name, align_bytes=64)
+            nc.scalar.copy(h[b][:], hbanks[b][:])
+
+        def gathers(b, first, stop, name):
+            terms = turns.tile([P, stop - first, V], F32, name=name, align_bytes=64)
+            for d in range(first, stop):
+                picked = terms[:, d - first, :]
                 gather(b, d, slice(0, V), picked)
                 for v in range(HALVES):
                     add_turned(early[v][:, b, :], picked[:, P * v : P * (v + 1)], d)
-        w2g = turns.tile([P, N, 4], BF16, name=f"wraw{BLOCKS - 1}_{LAST}", align_bytes=64)
+
+        project(grouped1, 1, 0, "wq0_2")
+        gathers(0, 0, 1, "terms0")
+        project(prepare(1, 2, 2, "ws0_2"), 1, 2)
+        gathers(0, 1, D, "wraw1_3")
+        grouped2 = prepare(2, 0, PASSES, "grouped2")
+        keep_h(1, "wraw2_3")
+        project(grouped2, 2, 0)
+        gathers(1, 0, 3, "terms1")
+        project(prepare(3, 0, PASSES, "grouped3"), 3, 0)
+        keep_h(2, "grouped3")
+        gathers(1, 3, D, "wraw3_3")
+        keep_h(3, "h3")
+        gathers(2, 0, D, "terms2")
+        w2g = turns.tile([P, N, 4], BF16, name="w2g", align_bytes=64)
         nc.scalar.copy(w2g[:], w2raw[:].rearrange("p t m -> p m t"))
         for v in range(HALVES):
             round_sums(nc.scalar.copy, 0, BLOCKS - 1, v, early[v][:].rearrange("r b i -> r (b i)"))

@@ -14,7 +14,7 @@ FLOPS = 2 * K * H * T + 2 * H * N * V
 BYTES = 4 * (K * T + K * H + H * N + D * V + N * V) + 2 * D * P * (V // 16)
 
 SCALAR_COLUMNS_WHOLE = 176
-SCALAR_COLUMNS_LAST = (128, 80)
+SCALAR_COLUMNS_LAST = (128, 128, 0)
 FINISH_AT = 2
 BEGIN_AT = 4
 SPLIT_LISTS = 2
@@ -41,11 +41,12 @@ def tile_picked_gcn_mlp_none_sub_l_kernel(tc, xT, w1, w2, gate, pos1, pos2, pos3
         pos = [lists.tile([P, V // 16], U16, name=f"pos{d}") for d in range(D)]
 
         xraw = [turns.tile([P, 4, T], F32, name=f"xraw{c}", align_bytes=64) for c in range(LAST)]
-        xlast = [turns.tile([P, 4, HT], F32, name=f"xlast{a}", align_bytes=64) for a in range(2)]
+        pieces = [slice(0, HT), slice(HT, HT + P), slice(HT + P, T)]
+        xlast = [turns.tile([P, 4, s.stop - s.start], F32, name=f"xlast{a}", align_bytes=64) for a, s in enumerate(pieces)]
         wraw = [[turns.tile([P, 4, P], F32, name=f"wraw{b}_{c}", align_bytes=64) for c in range(PASSES)] for b in range(BLOCKS)]
         w2raw = keep.tile([P, 4, N], F32, name="w2raw")
-        gate_rows = turns.tile([P, V], F32, name="xg", align_bytes=64)
-        nc.gpsimd.memset(gate_rows[: P - D, :], 0.0)
+        gate_rows = turns.tile([P, D // 2, V], F32, name="xg", align_bytes=64)
+        nc.gpsimd.memset(gate_rows[: P - 2], 0.0)
 
         def load_w1(b, c):
             nc.sync.dma_start(
@@ -57,20 +58,17 @@ def tile_picked_gcn_mlp_none_sub_l_kernel(tc, xT, w1, w2, gate, pos1, pos2, pos3
             nc.sync.dma_start(pos[d][:], lists_in[d])
 
         load_w1(0, 0)
-        nc.sync.dma_start(out=gate_rows[P - D : P - 2, :], in_=gate[0 : D - 2, 0, :])
-        nc.sync.dma_start(out=gate_rows[P - 2 :, :], in_=gate[D - 2 : D, 0, :])
+        nc.sync.dma_start(out=gate_rows[P - 2 :], in_=gate[:, 0, :].rearrange("(g e) v -> e g v", e=2))
+        load_list(0)
         load_w1(0, 1)
         for c in range(LAST):
             nc.sync.dma_start(out=xraw[c][:], in_=xT[512 * c : 512 * (c + 1), :].rearrange("(p j) w -> p j w", j=4))
         load_w1(0, 2)
         load_w1(0, 3)
-        for a in range(2):
-            nc.sync.dma_start(
-                out=xlast[a][:], in_=xT[512 * LAST :, HT * a : HT * (a + 1)].rearrange("(p j) w -> p j w", j=4)
-            )
+        for a, nodes in enumerate(pieces):
+            nc.sync.dma_start(out=xlast[a][:], in_=xT[512 * LAST :, nodes].rearrange("(p j) w -> p j w", j=4))
         load_w1(1, 0)
         load_w1(1, 1)
-        load_list(0)
         load_w1(1, 2)
         load_list(1)
         load_w1(1, 3)
@@ -84,30 +82,31 @@ def tile_picked_gcn_mlp_none_sub_l_kernel(tc, xT, w1, w2, gate, pos1, pos2, pos3
         ident = keep.tile([P, P], F32, name="ident")
         make_identity(nc, ident[:])
 
-        cols_bank = psum.tile([P, T], F32, name="zbank0")
+        gate_cols = keep.tile([P, HALVES, D // 2, 2], F32, name="gate_cols")
         for v in range(HALVES):
-            nc.tensor.transpose(cols_bank[:, P * v : P * (v + 1)], gate_rows[:, P * v : P * (v + 1)], ident[:])
-        gate_cols = keep.tile([P, HALVES, D], F32, name="gate_cols")
-        nc.scalar.copy(gate_cols[:], cols_bank[:, :V].rearrange("p (v r) -> p v r", v=HALVES)[:, :, P - D :])
+            cols_bank = psum.tile([P, D // 2, P], F32, name=f"early{v}")
+            for g in range(D // 2):
+                nc.tensor.transpose(cols_bank[:, g, :], gate_rows[:, g, P * v : P * (v + 1)], ident[:])
+            nc.scalar.copy(gate_cols[:, v], cols_bank[:, :, P - 2 :])
         gate_banks = []
         for g, name in enumerate(("zbank1", "last0", "last1")):
             pair_bank = psum.tile([P, T], F32, name=name)
             for e in range(2):
                 for v in range(HALVES):
-                    d = 2 * g + e
                     nc.tensor.transpose(
                         pair_bank[:, (2 * e + v) * P : (2 * e + v + 1) * P],
-                        gate_cols[:, v, d : d + 1].to_broadcast([P, P]),
+                        gate_cols[:, v, g, e : e + 1].to_broadcast([P, P]),
                         ident[:],
                     )
             gate_banks.append(pair_bank)
 
         gates = []
 
-        def keep_gates(g, name):
-            pair = turns.tile([P, 2, V], F32, name=name, align_bytes=64)
-            nc.scalar.copy(pair[:].rearrange("p e v -> p (e v)"), gate_banks[g][:])
-            gates.append(pair)
+        def keep_gates(first, stop, name):
+            pairs = turns.tile([P, stop - first, 2, V], F32, name=name, align_bytes=64)
+            for g in range(first, stop):
+                nc.scalar.copy(pairs[:, g - first].rearrange("p e v -> p (e v)"), gate_banks[g][:])
+                gates.append(pairs[:, g - first])
 
         def interleave(copy, grouped, raw):
             copy(grouped.rearrange("p (c i) t -> p c t i", i=4), raw.rearrange("p t (c i) -> p c t i", i=4))
@@ -129,15 +128,17 @@ def tile_picked_gcn_mlp_none_sub_l_kernel(tc, xT, w1, w2, gate, pos1, pos2, pos3
             nc.vector.quantize_mx(
                 out=codes[:].rearrange("p c w -> p (c w)").bitcast(FP8X4),
                 scales=scales[:].rearrange("p c w -> p (c w)"),
-                in_=grouped[:].rearrange("p c w t -> p (c w t)"),
+                in_=grouped.rearrange("p c w t -> p (c w t)"),
             )
             for e in range(count):
                 wq[b, first_pass + e] = (codes[:, e, :], scales[:, e, :])
 
         def quantise_x(c, raw, nodes, cut, name):
             grouped = turns.tile([P, nodes.stop - nodes.start, 4], BF16, name=name, align_bytes=64)
-            interleave(nc.scalar.copy, grouped[:, :cut, :], raw[:, :, :cut])
-            interleave(nc.vector.tensor_copy, grouped[:, cut:, :], raw[:, :, cut:])
+            if cut > 0:
+                interleave(nc.scalar.copy, grouped[:, :cut, :], raw[:, :, :cut])
+            if cut < nodes.stop - nodes.start:
+                interleave(nc.vector.tensor_copy, grouped[:, cut:, :], raw[:, :, cut:])
             nc.vector.quantize_mx(
                 out=xq[c][0][:, nodes].bitcast(FP8X4), scales=xq[c][1][:, nodes], in_=grouped[:].rearrange("p w t -> p (w t)")
             )
@@ -153,30 +154,26 @@ def tile_picked_gcn_mlp_none_sub_l_kernel(tc, xT, w1, w2, gate, pos1, pos2, pos3
                 stop=(c == LAST),
             )
 
-        keep_gates(0, "gates0")
-        grouped = turns.tile([P, 2, P, 4], BF16, name="xg", align_bytes=64)
+        grouped = turns.tile([P, 2, P, 4], BF16, name="grouped0_0", align_bytes=64)
         for c in range(2):
             interleave(nc.vector.tensor_copy, grouped[:, c], wraw[0][c][:])
-        quantise_w1(grouped, 0, 0)
-        pieces = [slice(0, HT), slice(HT, HT + P), slice(HT + P, T)]
+        quantise_w1(grouped[:], 0, 0)
         first_banks = [psum.tile([P, s.stop - s.start], F32, name=n) for s, n in zip(pieces, ("hbank0", "hbank1", "zbank0"))]
         for c in range(LAST):
             quantise_x(c, xraw[c], slice(0, T), SCALAR_COLUMNS_WHOLE, "xg")
-            if c + 1 < len(gate_banks):
-                keep_gates(c + 1, f"xraw{c}")
+            if c < 2:
+                keep_gates(*((0, 1), (1, 3))[c], f"xraw{c}")
             else:
                 grouped = turns.tile([P, 2, P, 4], BF16, name=f"xraw{c}", align_bytes=64)
                 interleave(nc.scalar.copy, grouped[:, 0], wraw[0][2][:])
                 interleave(nc.vector.tensor_copy, grouped[:, 1], wraw[0][3][:])
-                quantise_w1(grouped, 0, 2)
+                quantise_w1(grouped[:], 0, 2)
             for bank, nodes in zip(first_banks, pieces):
                 multiply(bank[:], 0, c, nodes)
-        quantise_x(LAST, xlast[0], slice(0, HT), SCALAR_COLUMNS_LAST[0], "xg")
-        multiply(first_banks[0][:], 0, LAST, pieces[0])
-        quantise_x(LAST, xlast[1], slice(HT, T), SCALAR_COLUMNS_LAST[1], "xlast0")
-        for bank, nodes in zip(first_banks[1:], pieces[1:]):
-            multiply(bank[:], 0, LAST, nodes)
-        grouped1 = turns.tile([P, 2, P, 4], BF16, name="xlast1", align_bytes=64)
+        for a, name in enumerate(("xg", "xlast0", "xg")):
+            quantise_x(LAST, xlast[a], pieces[a], SCALAR_COLUMNS_LAST[a], name)
+            multiply(first_banks[a][:], 0, LAST, pieces[a])
+        grouped1 = turns.tile([P, 2, P, 4], BF16, name="xlast2", align_bytes=64)
         interleave(nc.vector.tensor_copy, grouped1[:, 0], wraw[1][0][:])
         interleave(nc.vector.tensor_copy, grouped1[:, 1], wraw[1][1][:])
         h[0] = turns.tile([P, T], F32, name="h0", align_bytes=64)
@@ -207,7 +204,7 @@ def tile_picked_gcn_mlp_none_sub_l_kernel(tc, xT, w1, w2, gate, pos1, pos2, pos3
             grouped = turns.tile([P, count, P, 4], BF16, name=name, align_bytes=64)
             for e in range(count):
                 interleave(nc.scalar.copy, grouped[:, e], wraw[coming][first_pass + e][:])
-            return grouped
+            return grouped[:]
 
         def project(grouped, coming, first_pass, name=None):
             quantise_w1(grouped, coming, first_pass, name)
@@ -228,17 +225,20 @@ def tile_picked_gcn_mlp_none_sub_l_kernel(tc, xT, w1, w2, gate, pos1, pos2, pos3
                 for v in range(HALVES):
                     add_turned(early[v][:, b, :], picked[:, P * v : P * (v + 1)], d)
 
-        project(grouped1, 1, 0, "wq0_2")
+        project(grouped1[:], 1, 0, "wq0_2")
         gathers(0, 0, 1, "terms0")
-        project(prepare(1, 2, 2, "ws0_2"), 1, 2)
-        gathers(0, 1, D, "wraw1_3")
-        grouped2 = prepare(2, 0, PASSES, "grouped2")
+        late1 = prepare(1, 2, 2, "ws0_2")
+        project(late1[:, 0:1], 1, 2)
+        gathers(0, 1, 2, "wraw1_2")
+        project(late1[:, 1:2], 1, 3)
+        gathers(0, 2, D, "wraw1_3")
+        grouped2 = prepare(2, 0, PASSES, "xlast2")
         keep_h(1, "wraw2_3")
         project(grouped2, 2, 0)
-        gathers(1, 0, 3, "terms1")
-        project(prepare(3, 0, PASSES, "grouped3"), 3, 0)
-        keep_h(2, "grouped3")
-        gathers(1, 3, D, "wraw3_3")
+        gathers(1, 0, 4, "terms1")
+        project(prepare(3, 0, PASSES, "wraw2_2"), 3, 0)
+        keep_h(2, "wraw2_2")
+        gathers(1, 4, D, "wraw3_3")
         keep_h(3, "h3")
         gathers(2, 0, D, "terms2")
         w2g = turns.tile([P, N, 4], BF16, name="w2g", align_bytes=64)

@@ -59,7 +59,6 @@ def tile_picked_gcn_mlp_none_sub_l_kernel(tc, xT, w1, w2, gate, pos1, pos2, pos3
 
         load_w1(0, 0)
         nc.sync.dma_start(out=gate_rows[P - 2 :], in_=gate[:, 0, :].rearrange("(g e) v -> e g v", e=2))
-        load_list(0)
         load_w1(0, 1)
         for c in range(LAST):
             nc.sync.dma_start(out=xraw[c][:], in_=xT[512 * c : 512 * (c + 1), :].rearrange("(p j) w -> p j w", j=4))
@@ -69,12 +68,13 @@ def tile_picked_gcn_mlp_none_sub_l_kernel(tc, xT, w1, w2, gate, pos1, pos2, pos3
             nc.sync.dma_start(out=xlast[a][:], in_=xT[512 * LAST :, nodes].rearrange("(p j) w -> p j w", j=4))
         load_w1(1, 0)
         load_w1(1, 1)
+        load_list(0)
         load_w1(1, 2)
-        load_list(1)
         load_w1(1, 3)
+        for d in range(1, D):
+            load_list(d)
         for c in range(PASSES):
             load_w1(2, c)
-            load_list(2 + c)
         for c in range(PASSES):
             load_w1(3, c)
         nc.sync.dma_start(out=w2raw[:], in_=w2.rearrange("(p j) m -> p j m", j=4))
@@ -232,13 +232,16 @@ def tile_picked_gcn_mlp_none_sub_l_kernel(tc, xT, w1, w2, gate, pos1, pos2, pos3
         gathers(0, 1, 2, "wraw1_2")
         project(late1[:, 1:2], 1, 3)
         gathers(0, 2, D, "wraw1_3")
-        grouped2 = prepare(2, 0, PASSES, "xlast2")
-        keep_h(1, "wraw2_3")
-        project(grouped2, 2, 0)
-        gathers(1, 0, 4, "terms1")
-        project(prepare(3, 0, PASSES, "wraw2_2"), 3, 0)
-        keep_h(2, "wraw2_2")
-        gathers(1, 4, D, "wraw3_3")
+        project(prepare(2, 0, 2, "xlast2"), 2, 0)
+        keep_h(1, "wraw2_1")
+        gathers(1, 0, 1, "terms1")
+        project(prepare(2, 2, 2, "wraw2_0"), 2, 2)
+        gathers(1, 1, 3, "wraw2_3")
+        project(prepare(3, 0, 2, "wraw2_2"), 3, 0)
+        gathers(1, 3, D, "wraw3_1")
+        late3 = prepare(3, 2, 2, "wraw3_0")
+        keep_h(2, "wraw3_3")
+        project(late3, 3, 2)
         keep_h(3, "h3")
         gathers(2, 0, D, "terms2")
         w2g = turns.tile([P, N, 4], BF16, name="w2g", align_bytes=64)

@@ -17,7 +17,8 @@ SCALAR_COLUMNS_WHOLE = 176
 SCALAR_COLUMNS_LAST = (128, 128, 0)
 FINISH_AT = 2
 BEGIN_AT = 4
-SPLIT_LISTS = 2
+FUSED = 2
+PLAIN = D - FUSED
 
 F32 = mybir.dt.float32
 BF16 = mybir.dt.bfloat16
@@ -26,6 +27,7 @@ U16 = mybir.dt.uint16
 U8 = mybir.dt.uint8
 FP8X4 = mybir.dt.float8_e4m3fn_x4
 MULT = mybir.AluOpType.mult
+COPY = mybir.ActivationFunctionType.Copy
 
 
 def tile_picked_gcn_mlp_none_sub_l_kernel(tc, xT, w1, w2, gate, pos1, pos2, pos3, pos4, pos5, pos6, out):
@@ -237,37 +239,61 @@ def tile_picked_gcn_mlp_none_sub_l_kernel(tc, xT, w1, w2, gate, pos1, pos2, pos3
         gathers(1, 0, 1, "terms1")
         project(prepare(2, 2, 2, "wraw2_0"), 2, 2)
         gathers(1, 1, 3, "wraw2_3")
-        project(prepare(3, 0, 2, "wraw2_2"), 3, 0)
-        gathers(1, 3, D, "wraw3_1")
+        early3 = prepare(3, 0, 2, "wraw2_2")
         late3 = prepare(3, 2, 2, "wraw3_0")
-        keep_h(2, "wraw3_3")
+        project(early3, 3, 0)
+        gathers(1, 3, 4, "wraw3_1")
         project(late3, 3, 2)
+        behind = turns.tile([P, 2 + PLAIN, V], F32, name="wraw3_3", align_bytes=64)
+        for d in range(4, D):
+            gather(1, d, slice(0, V), behind[:, d - 4, :])
+            for v in range(HALVES):
+                add_turned(early[v][:, 1, :], behind[:, d - 4, P * v : P * (v + 1)], d)
+        keep_h(2, "wraw3_2")
+
+        def gather_plain(b, picked):
+            for d in range(FUSED, D):
+                nc.scalar.activation(picked[:, d - FUSED, :], h[b][:].indirect(pos[d][:]), COPY)
+
+        def weigh(picked, g, targets, sums, name):
+            width = targets.stop - targets.start
+            terms = keep.tile([P, 2, width], F32, name=name)
+            nc.vector.tensor_tensor(terms[:], picked[:, :, targets], gates[g][:, :, targets], MULT)
+            for e in range(2):
+                for v in range(targets.start // P, targets.stop // P):
+                    add_turned(sums[v], terms[:, e, P * v - targets.start : P * (v + 1) - targets.start], 2 * g + e)
+
+        last = BLOCKS - 1
+        plain2 = behind[:, 2:, :]
+        gather_plain(2, plain2)
         keep_h(3, "h3")
-        gathers(2, 0, D, "terms2")
+        plain3 = keep.tile([P, PLAIN, V], F32, name="plain3")
+        gather_plain(last, plain3)
+        gathers(2, 0, FUSED, "terms2")
+        for g in range(FUSED // 2, D // 2):
+            weigh(plain2[:, 2 * g - FUSED : 2 * g - FUSED + 2, :], g, slice(0, V), [early[v][:, 2, :] for v in range(HALVES)], f"weighed2_{g}")
         w2g = turns.tile([P, N, 4], BF16, name="w2g", align_bytes=64)
         nc.scalar.copy(w2g[:], w2raw[:].rearrange("p t m -> p m t"))
         for v in range(HALVES):
             round_sums(nc.scalar.copy, 0, BLOCKS - 1, v, early[v][:].rearrange("r b i -> r (b i)"))
 
-        last = BLOCKS - 1
         zbank = [psum.tile([P, 2, P], F32, name=f"zbank{v}") for v in range(HALVES)]
         zg = [keep.tile([P, P, 4], BF16, name=f"zg{v}", align_bytes=64) for v in range(HALVES)]
         zq = [keep.tile([P, P], U32, name=f"zq{v}", align_bytes=64) for v in range(HALVES)]
         zs = [keep.tile([P, P], U8, name=f"zs{v}", align_bytes=64) for v in range(HALVES)]
         result = [keep.tile([P, P], F32, name=f"result{v}") for v in range(HALVES)]
         last_sums = [psum.tile([P, P], F32, name=f"last{v}") for v in range(HALVES)]
+        last_views = [last_sums[v][:] for v in range(HALVES)]
 
-        for d in range(D - SPLIT_LISTS):
+        for d in range(FUSED):
             whole = keep.tile([P, V], F32, name=f"whole{d}")
             gather(last, d, slice(0, V), whole[:])
             for v in range(HALVES):
                 add_turned(last_sums[v][:], whole[:, P * v : P * (v + 1)], d)
+        weigh(plain3[:, 0:2, :], 1, slice(0, V), last_views, "weighed3_1")
 
         def gather_half(v):
-            for d in range(D - SPLIT_LISTS, D):
-                half = keep.tile([P, P], F32, name=f"half{d}_{v}")
-                gather(last, d, slice(P * v, P * (v + 1)), half[:])
-                add_turned(last_sums[v][:], half[:], d)
+            weigh(plain3[:, 2:4, :], 2, slice(P * v, P * (v + 1)), last_views, f"weighed3_2_{v}")
 
         def turn_back(v):
             words = zT[v][:].rearrange("r u p e -> r (u p e)").bitcast(F32)

@@ -251,29 +251,28 @@ def tile_picked_gcn_mlp_none_sub_l_kernel(tc, xT, w1, w2, gate, pos1, pos2, pos3
                 add_turned(early[v][:, 1, :], behind[:, d - 4, P * v : P * (v + 1)], d)
         keep_h(2, "wraw3_2")
 
-        def gather_plain(b, picked):
-            for d in range(FUSED, D):
+        def gather_plain(b, first, picked):
+            for d in range(first, D):
                 nc.scalar.activation(picked[:, d - FUSED, :], h[b][:].indirect(pos[d][:]), COPY)
 
-        def weigh(picked, g, targets, sums, name):
+        def weigh(picked, first, stop, targets, sums, name):
             width = targets.stop - targets.start
-            terms = keep.tile([P, 2, width], F32, name=name)
-            nc.vector.tensor_tensor(terms[:], picked[:, :, targets], gates[g][:, :, targets], MULT)
-            for e in range(2):
+            terms = turns.tile([P, stop - first, width], F32, name=name, align_bytes=64)
+            weights = gates[first // 2][:, first % 2 : first % 2 + stop - first, targets]
+            nc.vector.tensor_tensor(terms[:], picked[:, first - FUSED : stop - FUSED, targets], weights, MULT)
+            for d in range(first, stop):
                 for v in range(targets.start // P, targets.stop // P):
-                    add_turned(sums[v], terms[:, e, P * v - targets.start : P * (v + 1) - targets.start], 2 * g + e)
+                    add_turned(sums[v], terms[:, d - first, P * v - targets.start : P * (v + 1) - targets.start], d)
 
         last = BLOCKS - 1
         plain2 = behind[:, 2:, :]
-        gather_plain(2, plain2)
+        gather_plain(2, FUSED, plain2)
         keep_h(3, "h3")
-        plain3 = keep.tile([P, PLAIN, V], F32, name="plain3")
-        gather_plain(last, plain3)
+        plain3 = turns.tile([P, PLAIN, V], F32, name="plain3", align_bytes=64)
+        gather_plain(last, FUSED + 1, plain3)
         gathers(2, 0, FUSED, "terms2")
         for g in range(FUSED // 2, D // 2):
-            weigh(plain2[:, 2 * g - FUSED : 2 * g - FUSED + 2, :], g, slice(0, V), [early[v][:, 2, :] for v in range(HALVES)], f"weighed2_{g}")
-        w2g = turns.tile([P, N, 4], BF16, name="w2g", align_bytes=64)
-        nc.scalar.copy(w2g[:], w2raw[:].rearrange("p t m -> p m t"))
+            weigh(plain2, 2 * g, 2 * g + 2, slice(0, V), [early[v][:, 2, :] for v in range(HALVES)], f"weighed2_{g}")
         for v in range(HALVES):
             round_sums(nc.scalar.copy, 0, BLOCKS - 1, v, early[v][:].rearrange("r b i -> r (b i)"))
 
@@ -285,15 +284,15 @@ def tile_picked_gcn_mlp_none_sub_l_kernel(tc, xT, w1, w2, gate, pos1, pos2, pos3
         last_sums = [psum.tile([P, P], F32, name=f"last{v}") for v in range(HALVES)]
         last_views = [last_sums[v][:] for v in range(HALVES)]
 
-        for d in range(FUSED):
+        for d in range(FUSED + 1):
             whole = keep.tile([P, V], F32, name=f"whole{d}")
             gather(last, d, slice(0, V), whole[:])
             for v in range(HALVES):
                 add_turned(last_sums[v][:], whole[:, P * v : P * (v + 1)], d)
-        weigh(plain3[:, 0:2, :], 1, slice(0, V), last_views, "weighed3_1")
+        weigh(plain3, 3, 4, slice(0, V), last_views, "weighed3_1")
 
         def gather_half(v):
-            weigh(plain3[:, 2:4, :], 2, slice(P * v, P * (v + 1)), last_views, f"weighed3_2_{v}")
+            weigh(plain3, 4, 6, slice(P * v, P * (v + 1)), last_views, f"weighed3_2_{v}")
 
         def turn_back(v):
             words = zT[v][:].rearrange("r u p e -> r (u p e)").bitcast(F32)
@@ -323,9 +322,11 @@ def tile_picked_gcn_mlp_none_sub_l_kernel(tc, xT, w1, w2, gate, pos1, pos2, pos3
         round_sums(nc.scalar.copy, last, 1, 0, last_sums[0][:])
         turn_back(0)
         gather_half(1)
-        w2q = turns.tile([P, N], U32, name=f"h{last}", align_bytes=64)
-        nc.vector.quantize_mx(out=w2q[:].bitcast(FP8X4), scales=w2s[:], in_=w2g[:].rearrange("p m t -> p (m t)"))
-        second_layer(0, nc.scalar.copy)
+        w2g = turns.tile([P, N, 4], BF16, name="plain3", align_bytes=64)
+        interleave(nc.vector.tensor_copy, w2g[:], w2raw[:])
         round_sums(nc.vector.tensor_copy, last, 1, 1, last_sums[1][:])
         turn_back(1)
+        w2q = turns.tile([P, N], U32, name="weighed3_2_1", align_bytes=64)
+        nc.vector.quantize_mx(out=w2q[:].bitcast(FP8X4), scales=w2s[:], in_=w2g[:].rearrange("p m t -> p (m t)"))
+        second_layer(0, nc.scalar.copy)
         second_layer(1, nc.vector.tensor_copy)

@@ -72,8 +72,9 @@ def tile_picked_gcn_mlp_none_sub_l_kernel(tc, xT, w1, w2, gate, pos1, pos2, pos3
         load_w1(1, 1)
         load_list(0)
         load_w1(1, 2)
+        load_list(D - 1)
         load_w1(1, 3)
-        for d in range(1, D):
+        for d in range(1, D - 1):
             load_list(d)
         for c in range(PASSES):
             load_w1(2, c)
@@ -227,30 +228,6 @@ def tile_picked_gcn_mlp_none_sub_l_kernel(tc, xT, w1, w2, gate, pos1, pos2, pos3
                 for v in range(HALVES):
                     add_turned(early[v][:, b, :], picked[:, P * v : P * (v + 1)], d)
 
-        project(grouped1[:], 1, 0, "wq0_2")
-        gathers(0, 0, 1, "terms0")
-        late1 = prepare(1, 2, 2, "ws0_2")
-        project(late1[:, 0:1], 1, 2)
-        gathers(0, 1, 2, "wraw1_2")
-        project(late1[:, 1:2], 1, 3)
-        gathers(0, 2, D, "wraw1_3")
-        project(prepare(2, 0, 2, "xlast2"), 2, 0)
-        keep_h(1, "wraw2_1")
-        gathers(1, 0, 1, "terms1")
-        project(prepare(2, 2, 2, "wraw2_0"), 2, 2)
-        gathers(1, 1, 3, "wraw2_3")
-        early3 = prepare(3, 0, 2, "wraw2_2")
-        late3 = prepare(3, 2, 2, "wraw3_0")
-        project(early3, 3, 0)
-        gathers(1, 3, 4, "wraw3_1")
-        project(late3, 3, 2)
-        behind = turns.tile([P, 2 + PLAIN, V], F32, name="wraw3_3", align_bytes=64)
-        for d in range(4, D):
-            gather(1, d, slice(0, V), behind[:, d - 4, :])
-            for v in range(HALVES):
-                add_turned(early[v][:, 1, :], behind[:, d - 4, P * v : P * (v + 1)], d)
-        keep_h(2, "wraw3_2")
-
         def gather_plain(b, first, picked):
             for d in range(first, D):
                 nc.scalar.activation(picked[:, d - FUSED, :], h[b][:].indirect(pos[d][:]), COPY)
@@ -263,6 +240,36 @@ def tile_picked_gcn_mlp_none_sub_l_kernel(tc, xT, w1, w2, gate, pos1, pos2, pos3
             for d in range(first, stop):
                 for v in range(targets.start // P, targets.stop // P):
                     add_turned(sums[v], terms[:, d - first, P * v - targets.start : P * (v + 1) - targets.start], d)
+
+        def gathers_into(b, first, stop, terms):
+            for d in range(first, stop):
+                gather(b, d, slice(0, V), terms[:, d - first, :])
+                for v in range(HALVES):
+                    add_turned(early[v][:, b, :], terms[:, d - first, P * v : P * (v + 1)], d)
+
+        project(grouped1[:], 1, 0, "wq0_2")
+        gathers(0, 0, 1, "terms0")
+        late1 = prepare(1, 2, 2, "ws0_2")
+        project(late1[:, 0:1], 1, 2)
+        shared = turns.tile([P, PLAIN, V], F32, name="wraw1_2", align_bytes=64)
+        gather_plain(0, D - 1, shared)
+        gathers_into(0, 1, 3, shared)
+        project(late1[:, 1:2], 1, 3)
+        gathers(0, 3, 5, "wraw1_3")
+        weigh(shared, D - 1, D, slice(0, V), [early[v][:, 0, :] for v in range(HALVES)], "weighed0")
+        project(prepare(2, 0, 2, "xlast2"), 2, 0)
+        keep_h(1, "wraw2_1")
+        gathers(1, 0, 2, "terms1")
+        project(prepare(2, 2, 2, "wraw2_0"), 2, 2)
+        gathers(1, 2, 4, "wraw2_3")
+        early3 = prepare(3, 0, 2, "wraw2_2")
+        late3 = prepare(3, 2, 2, "wraw3_0")
+        project(early3, 3, 0)
+        gathers(1, 4, 5, "wraw3_1")
+        project(late3, 3, 2)
+        behind = turns.tile([P, 2 + PLAIN, V], F32, name="wraw3_3", align_bytes=64)
+        gathers_into(1, 5, 6, behind)
+        keep_h(2, "wraw3_2")
 
         last = BLOCKS - 1
         plain2 = behind[:, 2:, :]

@@ -27,6 +27,7 @@ U16 = mybir.dt.uint16
 U8 = mybir.dt.uint8
 FP8X4 = mybir.dt.float8_e4m3fn_x4
 MULT = mybir.AluOpType.mult
+ADD = mybir.AluOpType.add
 COPY = mybir.ActivationFunctionType.Copy
 
 
@@ -70,13 +71,14 @@ def tile_picked_gcn_mlp_none_sub_l_kernel(tc, xT, w1, w2, gate, pos1, pos2, pos3
             nc.sync.dma_start(out=xlast[a][:], in_=xT[512 * LAST :, nodes].rearrange("(p j) w -> p j w", j=4))
         load_w1(1, 0)
         load_w1(1, 1)
-        load_list(0)
         load_w1(1, 2)
-        load_list(D - 1)
+        load_list(0)
         load_w1(1, 3)
-        for d in range(1, D - 1):
+        for d in (1, 5, 2, 3):
             load_list(d)
-        for c in range(PASSES):
+        load_w1(2, 0)
+        load_list(4)
+        for c in range(1, PASSES):
             load_w1(2, c)
         for c in range(PASSES):
             load_w1(3, c)
@@ -191,8 +193,8 @@ def tile_picked_gcn_mlp_none_sub_l_kernel(tc, xT, w1, w2, gate, pos1, pos2, pos3
                 picked, h[b][:].indirect(pos[d][:, targets.start // 16 : targets.stop // 16]), gates[d // 2][:, d % 2, targets], MULT
             )
 
-        def add_turned(acc, picked, d):
-            nc.tensor.matmul(acc, picked, ident[:], is_transpose=True, start=(d == 0), stop=(d == D - 1))
+        def add_turned(acc, picked, d, count):
+            nc.tensor.matmul(acc, picked, ident[:], is_transpose=True, start=(d == 0), stop=(d == count - 1))
 
         def round_sums(copy, first_block, blocks, v, acc):
             copy(
@@ -220,86 +222,116 @@ def tile_picked_gcn_mlp_none_sub_l_kernel(tc, xT, w1, w2, gate, pos1, pos2, pos3
             h[b] = turns.tile([P, T], F32, name=name, align_bytes=64)
             nc.scalar.copy(h[b][:], hbanks[b][:])
 
-        def gathers(b, first, stop, name):
+        added = [0] * BLOCKS
+        last = BLOCKS - 1
+        last_sums = [psum.tile([P, P], F32, name=f"last{v}") for v in range(HALVES)]
+        sums = [[early[v][:, b, :] for v in range(HALVES)] for b in range(last)] + [[last_sums[v][:] for v in range(HALVES)]]
+
+        def add_term(b, term):
+            for v in range(HALVES):
+                add_turned(sums[b][v], term[:, P * v : P * (v + 1)], added[b], D if b == last else D - 1)
+            added[b] = added[b] + 1
+
+        def gated(b, d, name):
+            term = turns.tile([P, V], F32, name=name, align_bytes=64)
+            gather(b, d, slice(0, V), term[:])
+            add_term(b, term[:])
+
+        def gated_run(b, first, stop, name):
             terms = turns.tile([P, stop - first, V], F32, name=name, align_bytes=64)
             for d in range(first, stop):
-                picked = terms[:, d - first, :]
-                gather(b, d, slice(0, V), picked)
-                for v in range(HALVES):
-                    add_turned(early[v][:, b, :], picked[:, P * v : P * (v + 1)], d)
-
-        def gather_plain(b, first, picked):
-            for d in range(first, D):
-                nc.scalar.activation(picked[:, d - FUSED, :], h[b][:].indirect(pos[d][:]), COPY)
-
-        def weigh(picked, first, stop, targets, sums, name):
-            width = targets.stop - targets.start
-            terms = turns.tile([P, stop - first, width], F32, name=name, align_bytes=64)
-            weights = gates[first // 2][:, first % 2 : first % 2 + stop - first, targets]
-            nc.vector.tensor_tensor(terms[:], picked[:, first - FUSED : stop - FUSED, targets], weights, MULT)
-            for d in range(first, stop):
-                for v in range(targets.start // P, targets.stop // P):
-                    add_turned(sums[v], terms[:, d - first, P * v - targets.start : P * (v + 1) - targets.start], d)
-
-        def gathers_into(b, first, stop, terms):
-            for d in range(first, stop):
                 gather(b, d, slice(0, V), terms[:, d - first, :])
-                for v in range(HALVES):
-                    add_turned(early[v][:, b, :], terms[:, d - first, P * v : P * (v + 1)], d)
+                add_term(b, terms[:, d - first, :])
+
+        def plain(b, d, name):
+            picked = turns.tile([P, V], F32, name=name, align_bytes=64)
+            nc.scalar.activation(picked[:], h[b][:].indirect(pos[d][:]), COPY)
+            return picked
+
+        def weigh(b, d, picked, name):
+            term = turns.tile([P, V], F32, name=name, align_bytes=64)
+            nc.vector.tensor_tensor(term[:], picked[:], gates[d // 2][:, d % 2, :], MULT)
+            add_term(b, term[:])
+
+        cast_all = turns.tile([P, 10, P, 4], BF16, name="ws0_2", align_bytes=64)
+
+        def cast(b, c, count):
+            slot = PASSES * b + c - 6
+            for e in range(count):
+                interleave(nc.scalar.copy, cast_all[:, slot + e], wraw[b][c + e][:])
+            return cast_all[:, slot : slot + count]
+
+        raw_banks = [psum.tile([P, BLOCKS - 1, P], F32, name=f"zbank{v}") for v in range(HALVES)]
+
+        def turn_plain(b, name):
+            picked = plain(b, D - 1, name)
+            for v in range(HALVES):
+                nc.tensor.transpose(raw_banks[v][:, b, :], picked[:, P * v : P * (v + 1)], ident[:])
 
         project(grouped1[:], 1, 0, "wq0_2")
-        gathers(0, 0, 1, "terms0")
-        late1 = prepare(1, 2, 2, "ws0_2")
-        project(late1[:, 0:1], 1, 2)
-        shared = turns.tile([P, PLAIN, V], F32, name="wraw1_2", align_bytes=64)
-        gather_plain(0, D - 1, shared)
-        gathers_into(0, 1, 3, shared)
-        project(late1[:, 1:2], 1, 3)
-        gathers(0, 3, 5, "wraw1_3")
-        weigh(shared, D - 1, D, slice(0, V), [early[v][:, 0, :] for v in range(HALVES)], "weighed0")
-        project(prepare(2, 0, 2, "xlast2"), 2, 0)
+        gated(0, 0, "term00")
+        gated(0, 1, "term01")
+        project(cast(1, 2, 2), 1, 2)
+        turn_plain(0, "plain05")
+        gated_run(0, 2, 5, "wraw1_3")
+        project(cast(2, 0, 2), 2, 0)
         keep_h(1, "wraw2_1")
-        gathers(1, 0, 2, "terms1")
-        project(prepare(2, 2, 2, "wraw2_0"), 2, 2)
-        gathers(1, 2, 4, "wraw2_3")
-        early3 = prepare(3, 0, 2, "wraw2_2")
-        late3 = prepare(3, 2, 2, "wraw3_0")
+        gated(1, 0, "term10")
+        late2 = cast(2, 2, 2)
+        gated(1, 1, "wraw2_2")
+        project(late2, 2, 2)
+        gated(1, 2, "wraw2_3")
+        early3 = cast(3, 0, 2)
+        gated(1, 3, "wraw3_0")
         project(early3, 3, 0)
-        gathers(1, 4, 5, "wraw3_1")
-        project(late3, 3, 2)
-        behind = turns.tile([P, 2 + PLAIN, V], F32, name="wraw3_3", align_bytes=64)
-        gathers_into(1, 5, 6, behind)
-        keep_h(2, "wraw3_2")
-
-        last = BLOCKS - 1
-        plain2 = behind[:, 2:, :]
-        gather_plain(2, FUSED, plain2)
+        keep_h(2, "wraw3_1")
+        gated(1, 4, "term10")
+        gated(2, 0, "term20")
+        project(cast(3, 2, 2), 3, 2)
+        behind = turns.tile([P, 3, V], F32, name="wraw3_3", align_bytes=64)
+        for d in range(1, 4):
+            gather(2, d, slice(0, V), behind[:, d - 1, :])
+            add_term(2, behind[:, d - 1, :])
+        turn_plain(1, "wraw3_2")
+        turn_plain(2, "plain25")
         keep_h(3, "h3")
-        plain3 = turns.tile([P, PLAIN, V], F32, name="plain3", align_bytes=64)
-        gather_plain(last, FUSED + 1, plain3)
-        gathers(2, 0, FUSED, "terms2")
-        for g in range(FUSED // 2, D // 2):
-            weigh(plain2, 2 * g, 2 * g + 2, slice(0, V), [early[v][:, 2, :] for v in range(HALVES)], f"weighed2_{g}")
+        p24 = plain(2, 4, "plain24")
+        p33 = plain(3, 3, "plain33")
+        pair = turns.tile([P, 2, V], F32, name="plain3", align_bytes=64)
+        for e in range(2):
+            nc.scalar.activation(pair[:, e, :], h[last][:].indirect(pos[4 + e][:]), COPY)
+        gated(3, 0, "term30")
+        weigh(2, 4, p24, "weighed24")
+        gated(3, 1, "wraw3_1")
+        weigh(3, 3, p33, "weighed33")
+        gated(3, 2, "weighed24")
+        scaled = turns.tile([P, HALVES, 2, 32 * last, 2], F32, name="plain33", align_bytes=64)
         for v in range(HALVES):
-            round_sums(nc.scalar.copy, 0, BLOCKS - 1, v, early[v][:].rearrange("r b i -> r (b i)"))
+            nc.scalar.activation(
+                scaled[:, v],
+                raw_banks[v][:].rearrange("r b (q u e) -> r u (b q) e", u=2, e=2),
+                COPY,
+                scale=gate_cols[:, v, (D - 1) // 2, (D - 1) % 2 : (D - 1) % 2 + 1],
+            )
+
+        def finish_early(v):
+            nc.vector.tensor_tensor(
+                zT[v][:, :, : 32 * last, :], early[v][:].rearrange("r b (q u e) -> r u (b q) e", u=2, e=2), scaled[:, v], ADD
+            )
 
         zbank = [psum.tile([P, 2, P], F32, name=f"zbank{v}") for v in range(HALVES)]
         zg = [keep.tile([P, P, 4], BF16, name=f"zg{v}", align_bytes=64) for v in range(HALVES)]
         zq = [keep.tile([P, P], U32, name=f"zq{v}", align_bytes=64) for v in range(HALVES)]
         zs = [keep.tile([P, P], U8, name=f"zs{v}", align_bytes=64) for v in range(HALVES)]
         result = [keep.tile([P, P], F32, name=f"result{v}") for v in range(HALVES)]
-        last_sums = [psum.tile([P, P], F32, name=f"last{v}") for v in range(HALVES)]
-        last_views = [last_sums[v][:] for v in range(HALVES)]
-
-        for d in range(FUSED + 1):
-            whole = keep.tile([P, V], F32, name=f"whole{d}")
-            gather(last, d, slice(0, V), whole[:])
-            for v in range(HALVES):
-                add_turned(last_sums[v][:], whole[:, P * v : P * (v + 1)], d)
-        weigh(plain3, 3, 4, slice(0, V), last_views, "weighed3_1")
 
         def gather_half(v):
-            weigh(plain3, 4, 6, slice(P * v, P * (v + 1)), last_views, f"weighed3_2_{v}")
+            targets = slice(P * v, P * (v + 1))
+            terms = turns.tile([P, 2, P], F32, name=f"weighed3_2_{v}", align_bytes=64)
+            nc.vector.tensor_tensor(terms[:], pair[:, :, targets], gates[2][:, :, targets], MULT)
+            for e in range(2):
+                add_turned(last_sums[v][:], terms[:, e, :], D - 2 + e, D)
+            return terms
 
         def turn_back(v):
             words = zT[v][:].rearrange("r u p e -> r (u p e)").bitcast(F32)
@@ -326,14 +358,16 @@ def tile_picked_gcn_mlp_none_sub_l_kernel(tc, xT, w1, w2, gate, pos1, pos2, pos3
             nc.sync.dma_start(out=out[:, P * v : P * (v + 1)], in_=result[v][:])
 
         gather_half(0)
-        round_sums(nc.scalar.copy, last, 1, 0, last_sums[0][:])
-        turn_back(0)
         gather_half(1)
-        w2g = turns.tile([P, N, 4], BF16, name="plain3", align_bytes=64)
-        interleave(nc.vector.tensor_copy, w2g[:], w2raw[:])
-        round_sums(nc.vector.tensor_copy, last, 1, 1, last_sums[1][:])
+        finish_early(0)
+        round_sums(nc.scalar.copy, last, 1, 0, last_sums[0][:])
+        finish_early(1)
+        round_sums(nc.scalar.copy, last, 1, 1, last_sums[1][:])
+        turn_back(0)
         turn_back(1)
-        w2q = turns.tile([P, N], U32, name="weighed3_2_1", align_bytes=64)
+        w2g = turns.tile([P, N, 4], BF16, name="weighed3_2_1", align_bytes=64)
+        interleave(nc.vector.tensor_copy, w2g[:], w2raw[:])
+        w2q = turns.tile([P, N], U32, name="w2q", align_bytes=64)
         nc.vector.quantize_mx(out=w2q[:].bitcast(FP8X4), scales=w2s[:], in_=w2g[:].rearrange("p m t -> p (m t)"))
         second_layer(0, nc.scalar.copy)
         second_layer(1, nc.vector.tensor_copy)

@@ -28,6 +28,12 @@ U8 = mybir.dt.uint8
 FP8X4 = mybir.dt.float8_e4m3fn_x4
 MULT = mybir.AluOpType.mult
 ADD = mybir.AluOpType.add
+MAX = mybir.AluOpType.max
+IS_LT = mybir.AluOpType.is_lt
+AXIS_X = mybir.AxisListType.X
+PIVOT = 4
+SMALL = 2.0**-30
+FLOOR = 2.0**-120
 COPY = mybir.ActivationFunctionType.Copy
 
 
@@ -74,10 +80,10 @@ def tile_picked_gcn_mlp_none_sub_l_kernel(tc, xT, w1, w2, gate, pos1, pos2, pos3
         load_w1(1, 2)
         load_list(0)
         load_w1(1, 3)
-        for d in (1, 5, 2, 3):
+        for d in (1, PIVOT, 2, 3):
             load_list(d)
         load_w1(2, 0)
-        load_list(4)
+        load_list(5)
         for c in range(1, PASSES):
             load_w1(2, c)
         for c in range(PASSES):
@@ -93,25 +99,45 @@ def tile_picked_gcn_mlp_none_sub_l_kernel(tc, xT, w1, w2, gate, pos1, pos2, pos3
             for g in range(D // 2):
                 nc.tensor.transpose(cols_bank[:, g, :], gate_rows[:, g, P * v : P * (v + 1)], ident[:])
             nc.scalar.copy(gate_cols[:, v], cols_bank[:, :, P - 2 :])
+        weights = gate_cols[:].rearrange("r v g e -> r v (g e)")
+        top = keep.tile([P, HALVES], F32, name="top")
+        size = keep.tile([P, HALVES], F32, name="size")
+        bar = keep.tile([P, HALVES], F32, name="bar")
+        lift = keep.tile([P, HALVES], F32, name="lift")
+        pivot = keep.tile([P, HALVES], F32, name="pivot")
+        inverse = keep.tile([P, HALVES], F32, name="inverse")
+        ratio_cols = keep.tile([P, HALVES, D], F32, name="ratio_cols")
+        nc.vector.tensor_reduce(top[:], weights, AXIS_X, MAX, apply_absolute_value=True)
+        nc.vector.scalar_tensor_tensor(size[:], weights[:, :, PIVOT], -1.0, weights[:, :, PIVOT], MULT, MAX)
+        nc.vector.tensor_scalar(bar[:], top[:], SMALL, FLOOR, MULT, MAX)
+        for v in range(HALVES):
+            one = slice(v, v + 1)
+            nc.vector.scalar_tensor_tensor(lift[:, one], size[:, one], bar[:, one], bar[:, one], IS_LT, MULT)
+        nc.vector.scalar_tensor_tensor(pivot[:], lift[:], 2.0, weights[:, :, PIVOT], MULT, ADD)
+        nc.vector.reciprocal(inverse[:], pivot[:])
+        for v in range(HALVES):
+            nc.vector.tensor_scalar(ratio_cols[:, v], weights[:, v], inverse[:, v : v + 1], None, MULT)
         gate_banks = []
-        for g, name in enumerate(("zbank1", "last0", "last1")):
-            pair_bank = psum.tile([P, T], F32, name=name)
-            for e in range(2):
+        for pair, name in (((0, 1), "zbank1"), ((2, 3), "last0"), ((5,), "last1")):
+            pair_bank = psum.tile([P, len(pair), V], F32, name=name)
+            for e, d in enumerate(pair):
                 for v in range(HALVES):
                     nc.tensor.transpose(
-                        pair_bank[:, (2 * e + v) * P : (2 * e + v + 1) * P],
-                        gate_cols[:, v, g, e : e + 1].to_broadcast([P, P]),
-                        ident[:],
+                        pair_bank[:, e, v * P : (v + 1) * P], ratio_cols[:, v, d : d + 1].to_broadcast([P, P]), ident[:]
                     )
-            gate_banks.append(pair_bank)
+            gate_banks.append((pair, pair_bank))
 
-        gates = []
+        ratios = {}
 
         def keep_gates(first, stop, name):
-            pairs = turns.tile([P, stop - first, 2, V], F32, name=name, align_bytes=64)
-            for g in range(first, stop):
-                nc.scalar.copy(pairs[:, g - first].rearrange("p e v -> p (e v)"), gate_banks[g][:])
-                gates.append(pairs[:, g - first])
+            count = sum(len(pair) for pair, bank in gate_banks[first:stop])
+            kept = turns.tile([P, count, V], F32, name=name, align_bytes=64)
+            at = 0
+            for pair, bank in gate_banks[first:stop]:
+                nc.scalar.copy(kept[:, at : at + len(pair)], bank[:])
+                for e, d in enumerate(pair):
+                    ratios[d] = kept[:, at + e]
+                at = at + len(pair)
 
         def interleave(copy, grouped, raw):
             copy(grouped.rearrange("p (c i) t -> p c t i", i=4), raw.rearrange("p t (c i) -> p c t i", i=4))
@@ -166,9 +192,9 @@ def tile_picked_gcn_mlp_none_sub_l_kernel(tc, xT, w1, w2, gate, pos1, pos2, pos3
         first_banks = [psum.tile([P, s.stop - s.start], F32, name=n) for s, n in zip(pieces, ("hbank0", "hbank1", "zbank0"))]
         for c in range(LAST):
             quantise_x(c, xraw[c], slice(0, T), SCALAR_COLUMNS_WHOLE, "xg")
-            if c < 2:
-                keep_gates(*((0, 1), (1, 3))[c], f"xraw{c}")
-            else:
+            if c == 1:
+                keep_gates(0, 2, "xraw1")
+            if c == 2:
                 grouped = turns.tile([P, 2, P, 4], BF16, name=f"xraw{c}", align_bytes=64)
                 interleave(nc.scalar.copy, grouped[:, 0], wraw[0][2][:])
                 interleave(nc.vector.tensor_copy, grouped[:, 1], wraw[0][3][:])
@@ -178,6 +204,7 @@ def tile_picked_gcn_mlp_none_sub_l_kernel(tc, xT, w1, w2, gate, pos1, pos2, pos3
         for a, name in enumerate(("xg", "xlast0", "xg")):
             quantise_x(LAST, xlast[a], pieces[a], SCALAR_COLUMNS_LAST[a], name)
             multiply(first_banks[a][:], 0, LAST, pieces[a])
+        keep_gates(2, 3, "xlast1")
         grouped1 = turns.tile([P, 2, P, 4], BF16, name="xlast2", align_bytes=64)
         interleave(nc.vector.tensor_copy, grouped1[:, 0], wraw[1][0][:])
         interleave(nc.vector.tensor_copy, grouped1[:, 1], wraw[1][1][:])
@@ -186,23 +213,19 @@ def tile_picked_gcn_mlp_none_sub_l_kernel(tc, xT, w1, w2, gate, pos1, pos2, pos3
             copy(h[0][:, nodes], bank[:])
 
         w2s = keep.tile([P, N], U8, name="w2s", align_bytes=64)
-        zT = [keep.tile([P, 2, P, 2], BF16, name=f"zT{v}") for v in range(HALVES)]
 
         def gather(b, d, targets, picked):
-            nc.vector.tensor_tensor(
-                picked, h[b][:].indirect(pos[d][:, targets.start // 16 : targets.stop // 16]), gates[d // 2][:, d % 2, targets], MULT
-            )
+            window = h[b][:].indirect(pos[d][:, targets.start // 16 : targets.stop // 16])
+            if d == PIVOT:
+                nc.vector.tensor_copy(picked, window)
+            else:
+                nc.vector.tensor_tensor(picked, window, ratios[d][:, targets], MULT)
 
         def add_turned(acc, picked, d, count):
             nc.tensor.matmul(acc, picked, ident[:], is_transpose=True, start=(d == 0), stop=(d == count - 1))
 
-        def round_sums(copy, first_block, blocks, v, acc):
-            copy(
-                zT[v][:, :, 32 * first_block : 32 * (first_block + blocks), :],
-                acc.rearrange("r (q u e) -> r u q e", u=2, e=2),
-            )
-
-        early = [psum.tile([P, BLOCKS - 1, P], F32, name=f"early{v}") for v in range(HALVES)]
+        early = [psum.tile([P, 2, P], F32, name=f"early{v}") for v in range(HALVES)]
+        third = [psum.tile([P, P], F32, name=f"zbank{v}") for v in range(HALVES)]
         hbanks = {}
 
         def prepare(coming, first_pass, count, name):
@@ -225,11 +248,12 @@ def tile_picked_gcn_mlp_none_sub_l_kernel(tc, xT, w1, w2, gate, pos1, pos2, pos3
         added = [0] * BLOCKS
         last = BLOCKS - 1
         last_sums = [psum.tile([P, P], F32, name=f"last{v}") for v in range(HALVES)]
-        sums = [[early[v][:, b, :] for v in range(HALVES)] for b in range(last)] + [[last_sums[v][:] for v in range(HALVES)]]
+        sums = [[early[v][:, b, :] for v in range(HALVES)] for b in range(2)]
+        sums = sums + [[bank[:] for bank in banks] for banks in (third, last_sums)]
 
         def add_term(b, term):
             for v in range(HALVES):
-                add_turned(sums[b][v], term[:, P * v : P * (v + 1)], added[b], D if b == last else D - 1)
+                add_turned(sums[b][v], term[:, P * v : P * (v + 1)], added[b], D)
             added[b] = added[b] + 1
 
         def gated(b, d, name):
@@ -237,11 +261,11 @@ def tile_picked_gcn_mlp_none_sub_l_kernel(tc, xT, w1, w2, gate, pos1, pos2, pos3
             gather(b, d, slice(0, V), term[:])
             add_term(b, term[:])
 
-        def gated_run(b, first, stop, name):
-            terms = turns.tile([P, stop - first, V], F32, name=name, align_bytes=64)
-            for d in range(first, stop):
-                gather(b, d, slice(0, V), terms[:, d - first, :])
-                add_term(b, terms[:, d - first, :])
+        def gated_run(b, run, name):
+            terms = turns.tile([P, len(run), V], F32, name=name, align_bytes=64)
+            for e, d in enumerate(run):
+                gather(b, d, slice(0, V), terms[:, e, :])
+                add_term(b, terms[:, e, :])
 
         def plain(b, d, name):
             picked = turns.tile([P, V], F32, name=name, align_bytes=64)
@@ -250,7 +274,7 @@ def tile_picked_gcn_mlp_none_sub_l_kernel(tc, xT, w1, w2, gate, pos1, pos2, pos3
 
         def weigh(b, d, picked, name):
             term = turns.tile([P, V], F32, name=name, align_bytes=64)
-            nc.vector.tensor_tensor(term[:], picked[:], gates[d // 2][:, d % 2, :], MULT)
+            nc.vector.tensor_tensor(term[:], picked[:], ratios[d], MULT)
             add_term(b, term[:])
 
         cast_all = turns.tile([P, 10, P, 4], BF16, name="ws0_2", align_bytes=64)
@@ -261,19 +285,15 @@ def tile_picked_gcn_mlp_none_sub_l_kernel(tc, xT, w1, w2, gate, pos1, pos2, pos3
                 interleave(nc.scalar.copy, cast_all[:, slot + e], wraw[b][c + e][:])
             return cast_all[:, slot : slot + count]
 
-        raw_banks = [psum.tile([P, BLOCKS - 1, P], F32, name=f"zbank{v}") for v in range(HALVES)]
-
-        def turn_plain(b, name):
-            picked = plain(b, D - 1, name)
-            for v in range(HALVES):
-                nc.tensor.transpose(raw_banks[v][:, b, :], picked[:, P * v : P * (v + 1)], ident[:])
+        def pivot_term(b, name):
+            add_term(b, plain(b, PIVOT, name)[:])
 
         project(grouped1[:], 1, 0, "wq0_2")
         gated(0, 0, "term00")
         gated(0, 1, "term01")
         project(cast(1, 2, 2), 1, 2)
-        turn_plain(0, "plain05")
-        gated_run(0, 2, 5, "wraw1_3")
+        pivot_term(0, "plain04")
+        gated_run(0, (2, 3, 5), "wraw1_3")
         project(cast(2, 0, 2), 2, 0)
         keep_h(1, "wraw2_1")
         gated(1, 0, "term10")
@@ -285,39 +305,30 @@ def tile_picked_gcn_mlp_none_sub_l_kernel(tc, xT, w1, w2, gate, pos1, pos2, pos3
         gated(1, 3, "wraw3_0")
         project(early3, 3, 0)
         keep_h(2, "wraw3_1")
-        gated(1, 4, "term10")
+        gated(1, 5, "term10")
         gated(2, 0, "term20")
         project(cast(3, 2, 2), 3, 2)
-        behind = turns.tile([P, 3, V], F32, name="wraw3_3", align_bytes=64)
-        for d in range(1, 4):
-            gather(2, d, slice(0, V), behind[:, d - 1, :])
-            add_term(2, behind[:, d - 1, :])
-        turn_plain(1, "wraw3_2")
-        turn_plain(2, "plain25")
+        gated_run(2, (1, 2, 3), "wraw3_3")
+        p25 = plain(2, 5, "wraw3_2")
+        pivot_term(1, "plain14")
         keep_h(3, "h3")
-        p24 = plain(2, 4, "plain24")
+        weigh(2, 5, p25, "weighed25")
+        pivot_term(2, "plain24")
         p33 = plain(3, 3, "plain33")
-        pair = turns.tile([P, 2, V], F32, name="plain3", align_bytes=64)
-        for e in range(2):
-            nc.scalar.activation(pair[:, e, :], h[last][:].indirect(pos[4 + e][:]), COPY)
+        p35 = plain(3, 5, "plain35")
         gated(3, 0, "term30")
-        weigh(2, 4, p24, "weighed24")
         gated(3, 1, "wraw3_1")
         weigh(3, 3, p33, "weighed33")
-        gated(3, 2, "weighed24")
-        scaled = turns.tile([P, HALVES, 2, 32 * last, 2], F32, name="plain33", align_bytes=64)
-        for v in range(HALVES):
-            nc.scalar.activation(
-                scaled[:, v],
-                raw_banks[v][:].rearrange("r b (q u e) -> r u (b q) e", u=2, e=2),
-                COPY,
-                scale=gate_cols[:, v, (D - 1) // 2, (D - 1) % 2 : (D - 1) % 2 + 1],
-            )
+        weigh(3, 5, p35, "weighed35")
+        pivot_term(3, "plain34")
 
-        def finish_early(v):
-            nc.vector.tensor_tensor(
-                zT[v][:, :, : 32 * last, :], early[v][:].rearrange("r b (q u e) -> r u (b q) e", u=2, e=2), scaled[:, v], ADD
-            )
+        def round_sums(engine, v, first, blocks, bank):
+            to = zT[v][:, :, 32 * first : 32 * (first + blocks), :]
+            sums_v = bank.rearrange("r (q u e) -> r u q e", u=2, e=2)
+            if engine is nc.scalar:
+                nc.scalar.activation(to, sums_v, COPY, scale=pivot[:, v : v + 1])
+            else:
+                nc.vector.tensor_scalar(to, sums_v, pivot[:, v : v + 1], None, MULT)
 
         zbank = [psum.tile([P, 2, P], F32, name=f"zbank{v}") for v in range(HALVES)]
         zg = [keep.tile([P, P, 4], BF16, name=f"zg{v}", align_bytes=64) for v in range(HALVES)]
@@ -327,11 +338,9 @@ def tile_picked_gcn_mlp_none_sub_l_kernel(tc, xT, w1, w2, gate, pos1, pos2, pos3
 
         def gather_half(v):
             targets = slice(P * v, P * (v + 1))
-            terms = turns.tile([P, 2, P], F32, name=f"weighed3_2_{v}", align_bytes=64)
-            nc.vector.tensor_tensor(terms[:], pair[:, :, targets], gates[2][:, :, targets], MULT)
-            for e in range(2):
-                add_turned(last_sums[v][:], terms[:, e, :], D - 2 + e, D)
-            return terms
+            term = turns.tile([P, P], F32, name=f"last_term{v}", align_bytes=64)
+            gather(last, 2, targets, term[:])
+            add_turned(last_sums[v][:], term[:], D - 1, D)
 
         def turn_back(v):
             words = zT[v][:].rearrange("r u p e -> r (u p e)").bitcast(F32)
@@ -359,13 +368,15 @@ def tile_picked_gcn_mlp_none_sub_l_kernel(tc, xT, w1, w2, gate, pos1, pos2, pos3
 
         gather_half(0)
         gather_half(1)
-        finish_early(0)
-        round_sums(nc.scalar.copy, last, 1, 0, last_sums[0][:])
-        finish_early(1)
-        round_sums(nc.scalar.copy, last, 1, 1, last_sums[1][:])
+        zT = [turns.tile([P, 2, P, 2], BF16, name=n, align_bytes=64) for n in ("plain35", "h3")]
+        for v, engine in enumerate((nc.scalar, nc.vector)):
+            round_sums(engine, v, 0, 2, early[v][:].rearrange("r b c -> r (b c)"))
+            round_sums(engine, v, 2, 1, third[v][:])
+        round_sums(nc.scalar, 0, last, 1, last_sums[0][:])
+        round_sums(nc.scalar, 1, last, 1, last_sums[1][:])
         turn_back(0)
         turn_back(1)
-        w2g = turns.tile([P, N, 4], BF16, name="weighed3_2_1", align_bytes=64)
+        w2g = turns.tile([P, N, 4], BF16, name="last_term1", align_bytes=64)
         interleave(nc.vector.tensor_copy, w2g[:], w2raw[:])
         w2q = turns.tile([P, N], U32, name="w2q", align_bytes=64)
         nc.vector.quantize_mx(out=w2q[:].bitcast(FP8X4), scales=w2s[:], in_=w2g[:].rearrange("p m t -> p (m t)"))

@@ -312,6 +312,17 @@ def tile_picked_gcn_mlp_none_sub_l_kernel(tc, xT, w1, w2, gate, pos1, pos2, pos3
         p25 = plain(2, 5, "wraw3_2")
         pivot_term(1, "plain14")
         keep_h(3, "h3")
+        idle_bank = psum.tile([P, T], F32, name="hbank0")
+        for nodes in (slice(0, T), slice(0, HT)):
+            nc.tensor.matmul_mx(
+                out=idle_bank[:, nodes],
+                lhsT=wq[last, LAST][0].bitcast(FP8X4),
+                lhsT_scale=wq[last, LAST][1],
+                rhs=xq[LAST][0][:, nodes].bitcast(FP8X4),
+                rhs_scale=xq[LAST][1][:, nodes],
+                start=True,
+                stop=True,
+            )
         weigh(2, 5, p25, "weighed25")
         pivot_term(2, "plain24")
         p33 = plain(3, 3, "plain33")

@@ -225,7 +225,8 @@ def tile_picked_gcn_mlp_none_sub_l_kernel(tc, xT, w1, w2, gate, pos1, pos2, pos3
             nc.tensor.matmul(acc, picked, ident[:], is_transpose=True, start=(d == 0), stop=(d == count - 1))
 
         early = [psum.tile([P, 2, P], F32, name=f"early{v}") for v in range(HALVES)]
-        third = [psum.tile([P, P], F32, name=f"zbank{v}") for v in range(HALVES)]
+        third_banks = [psum.tile([P, T], F32, name=f"zbank{v}") for v in range(HALVES)]
+        third = [bank[:, :P] for bank in third_banks]
         hbanks = {}
 
         def prepare(coming, first_pass, count, name):
@@ -249,7 +250,7 @@ def tile_picked_gcn_mlp_none_sub_l_kernel(tc, xT, w1, w2, gate, pos1, pos2, pos3
         last = BLOCKS - 1
         last_sums = [psum.tile([P, P], F32, name=f"last{v}") for v in range(HALVES)]
         sums = [[early[v][:, b, :] for v in range(HALVES)] for b in range(2)]
-        sums = sums + [[bank[:] for bank in banks] for banks in (third, last_sums)]
+        sums = sums + [third, [bank[:] for bank in last_sums]]
 
         def add_term(b, term):
             for v in range(HALVES):
@@ -312,19 +313,19 @@ def tile_picked_gcn_mlp_none_sub_l_kernel(tc, xT, w1, w2, gate, pos1, pos2, pos3
         p25 = plain(2, 5, "wraw3_2")
         pivot_term(1, "plain14")
         keep_h(3, "h3")
-        idle_bank = psum.tile([P, T], F32, name="hbank0")
-        for nodes in (slice(0, T), slice(0, HT)):
-            nc.tensor.matmul_mx(
-                out=idle_bank[:, nodes],
-                lhsT=wq[last, LAST][0].bitcast(FP8X4),
-                lhsT_scale=wq[last, LAST][1],
-                rhs=xq[LAST][0][:, nodes].bitcast(FP8X4),
-                rhs_scale=xq[LAST][1][:, nodes],
-                start=True,
-                stop=True,
-            )
         weigh(2, 5, p25, "weighed25")
         pivot_term(2, "plain24")
+        for bank in third_banks:
+            for nodes in (slice(HT, T), slice(P, HT)):
+                nc.tensor.matmul_mx(
+                    out=bank[:, nodes],
+                    lhsT=wq[last, LAST][0].bitcast(FP8X4),
+                    lhsT_scale=wq[last, LAST][1],
+                    rhs=xq[LAST][0][:, nodes].bitcast(FP8X4),
+                    rhs_scale=xq[LAST][1][:, nodes],
+                    start=True,
+                    stop=True,
+                )
         p33 = plain(3, 3, "plain33")
         p35 = plain(3, 5, "plain35")
         gated(3, 0, "term30")
@@ -382,7 +383,7 @@ def tile_picked_gcn_mlp_none_sub_l_kernel(tc, xT, w1, w2, gate, pos1, pos2, pos3
         zT = [turns.tile([P, 2, P, 2], BF16, name=n, align_bytes=64) for n in ("plain35", "h3")]
         for v, engine in enumerate((nc.scalar, nc.vector)):
             round_sums(engine, v, 0, 2, early[v][:].rearrange("r b c -> r (b c)"))
-            round_sums(engine, v, 2, 1, third[v][:])
+            round_sums(engine, v, 2, 1, third[v])
         round_sums(nc.scalar, 0, last, 1, last_sums[0][:])
         round_sums(nc.scalar, 1, last, 1, last_sums[1][:])
         turn_back(0)

@@ -224,7 +224,7 @@ def tile_picked_gcn_mlp_none_sub_l_kernel(tc, xT, w1, w2, gate, pos1, pos2, pos3
         def add_turned(acc, picked, d, count):
             nc.tensor.matmul(acc, picked, ident[:], is_transpose=True, start=(d == 0), stop=(d == count - 1))
 
-        early = [psum.tile([P, 2, P], F32, name=f"early{v}") for v in range(HALVES)]
+        early = [psum.tile([P, 3, P], F32, name=f"early{v}") for v in range(HALVES)]
         third_banks = [psum.tile([P, T], F32, name=f"zbank{v}") for v in range(HALVES)]
         third = [bank[:, :P] for bank in third_banks]
         hbanks = {}
@@ -254,7 +254,7 @@ def tile_picked_gcn_mlp_none_sub_l_kernel(tc, xT, w1, w2, gate, pos1, pos2, pos3
 
         def add_term(b, term):
             for v in range(HALVES):
-                add_turned(sums[b][v], term[:, P * v : P * (v + 1)], added[b], D)
+                add_turned(sums[b][v], term[:, P * v : P * (v + 1)], added[b], D - 1 if b == 2 else D)
             added[b] = added[b] + 1
 
         def gated(b, d, name):
@@ -312,8 +312,9 @@ def tile_picked_gcn_mlp_none_sub_l_kernel(tc, xT, w1, w2, gate, pos1, pos2, pos3
         gated_run(2, (1, 2, 3), "wraw3_3")
         p25 = plain(2, 5, "wraw3_2")
         pivot_term(1, "plain14")
+        for v in range(HALVES):
+            nc.tensor.transpose(early[v][:, 2, :], p25[:, P * v : P * (v + 1)], ident[:])
         keep_h(3, "h3")
-        weigh(2, 5, p25, "weighed25")
         pivot_term(2, "plain24")
         for bank in third_banks:
             for nodes in (slice(HT, T), slice(P, HT)):
@@ -381,9 +382,17 @@ def tile_picked_gcn_mlp_none_sub_l_kernel(tc, xT, w1, w2, gate, pos1, pos2, pos3
         gather_half(0)
         gather_half(1)
         zT = [turns.tile([P, 2, P, 2], BF16, name=n, align_bytes=64) for n in ("plain35", "h3")]
-        for v, engine in enumerate((nc.scalar, nc.vector)):
-            round_sums(engine, v, 0, 2, early[v][:].rearrange("r b c -> r (b c)"))
-            round_sums(engine, v, 2, 1, third[v])
+        scaled = turns.tile([P, HALVES, 2, 32, 2], F32, name="plain33", align_bytes=64)
+        for v in range(HALVES):
+            nc.scalar.activation(
+                scaled[:, v], early[v][:, 2, :].rearrange("r (q u e) -> r u q e", u=2, e=2), COPY, scale=weights[:, v, 5:6]
+            )
+        for v, engine in ((1, nc.vector), (0, nc.scalar)):
+            round_sums(engine, v, 0, 2, early[v][:, :2].rearrange("r b c -> r (b c)"))
+        for v in range(HALVES):
+            sums_v = third[v].rearrange("r (q u e) -> r u q e", u=2, e=2)
+            for u in range(2):
+                nc.vector.scalar_tensor_tensor(zT[v][:, u, 64:96, :], sums_v[:, u], pivot[:, v : v + 1], scaled[:, v, u], MULT, ADD)
         round_sums(nc.scalar, 0, last, 1, last_sums[0][:])
         round_sums(nc.scalar, 1, last, 1, last_sums[1][:])
         turn_back(0)

@@ -15,10 +15,10 @@ BYTES = 4 * (K * T + K * H + H * N + D * V + N * V) + 2 * D * P * (V // 16)
 
 SCALAR_COLUMNS_WHOLE = 176
 SCALAR_COLUMNS_LAST = (128, 128, 0)
-FINISH_AT = 2
-BEGIN_AT = 4
-FUSED = 2
-PLAIN = D - FUSED
+PIVOT = 4
+APART = 5
+SMALL = 2.0**-30
+FLOOR = 2.0**-120
 
 F32 = mybir.dt.float32
 BF16 = mybir.dt.bfloat16
@@ -31,9 +31,6 @@ ADD = mybir.AluOpType.add
 MAX = mybir.AluOpType.max
 IS_LT = mybir.AluOpType.is_lt
 AXIS_X = mybir.AxisListType.X
-PIVOT = 4
-SMALL = 2.0**-30
-FLOOR = 2.0**-120
 COPY = mybir.ActivationFunctionType.Copy
 
 
@@ -83,7 +80,7 @@ def tile_picked_gcn_mlp_none_sub_l_kernel(tc, xT, w1, w2, gate, pos1, pos2, pos3
         for d in (1, PIVOT, 2, 3):
             load_list(d)
         load_w1(2, 0)
-        load_list(5)
+        load_list(APART)
         for c in range(1, PASSES):
             load_w1(2, c)
         for c in range(PASSES):
@@ -118,7 +115,7 @@ def tile_picked_gcn_mlp_none_sub_l_kernel(tc, xT, w1, w2, gate, pos1, pos2, pos3
         for v in range(HALVES):
             nc.vector.tensor_scalar(ratio_cols[:, v], weights[:, v], inverse[:, v : v + 1], None, MULT)
         gate_banks = []
-        for pair, name in (((0, 1), "zbank1"), ((2, 3), "last0"), ((5,), "last1")):
+        for pair, name in (((0, 1), "zbank1"), ((2, 3), "last0"), ((APART,), "last1")):
             pair_bank = psum.tile([P, len(pair), V], F32, name=name)
             for e, d in enumerate(pair):
                 for v in range(HALVES):
@@ -214,53 +211,27 @@ def tile_picked_gcn_mlp_none_sub_l_kernel(tc, xT, w1, w2, gate, pos1, pos2, pos3
 
         w2s = keep.tile([P, N], U8, name="w2s", align_bytes=64)
 
-        def gather(b, d, targets, picked):
-            window = h[b][:].indirect(pos[d][:, targets.start // 16 : targets.stop // 16])
-            if d == PIVOT:
-                nc.vector.tensor_copy(picked, window)
-            else:
-                nc.vector.tensor_tensor(picked, window, ratios[d][:, targets], MULT)
-
-        def add_turned(acc, picked, d, count):
-            nc.tensor.matmul(acc, picked, ident[:], is_transpose=True, start=(d == 0), stop=(d == count - 1))
-
         early = [psum.tile([P, 3, P], F32, name=f"early{v}") for v in range(HALVES)]
         third_banks = [psum.tile([P, T], F32, name=f"zbank{v}") for v in range(HALVES)]
-        third = [bank[:, :P] for bank in third_banks]
+        last = BLOCKS - 1
+        last_banks = [psum.tile([P, P], F32, name=f"last{v}") for v in range(HALVES)]
+        sums = [[early[v][:, b, :] for v in range(HALVES)] for b in range(2)]
+        sums = sums + [[bank[:, :P] for bank in third_banks], [bank[:] for bank in last_banks]]
+        count = (D, D, D - 1, D)
+        added = [0] * BLOCKS
         hbanks = {}
 
-        def prepare(coming, first_pass, count, name):
-            grouped = turns.tile([P, count, P, 4], BF16, name=name, align_bytes=64)
-            for e in range(count):
-                interleave(nc.scalar.copy, grouped[:, e], wraw[coming][first_pass + e][:])
-            return grouped[:]
-
-        def project(grouped, coming, first_pass, name=None):
-            quantise_w1(grouped, coming, first_pass, name)
-            if first_pass == 0:
-                hbanks[coming] = psum.tile([P, T], F32, name=f"hbank{(coming + 1) % 2}")
-            for e in range(grouped.shape[1]):
-                multiply(hbanks[coming][:], coming, first_pass + e, slice(0, T))
-
-        def keep_h(b, name):
-            h[b] = turns.tile([P, T], F32, name=name, align_bytes=64)
-            nc.scalar.copy(h[b][:], hbanks[b][:])
-
-        added = [0] * BLOCKS
-        last = BLOCKS - 1
-        last_sums = [psum.tile([P, P], F32, name=f"last{v}") for v in range(HALVES)]
-        sums = [[early[v][:, b, :] for v in range(HALVES)] for b in range(2)]
-        sums = sums + [third, [bank[:] for bank in last_sums]]
+        def add_turned(acc, picked, place, terms):
+            nc.tensor.matmul(acc, picked, ident[:], is_transpose=True, start=(place == 0), stop=(place == terms - 1))
 
         def add_term(b, term):
             for v in range(HALVES):
-                add_turned(sums[b][v], term[:, P * v : P * (v + 1)], added[b], D - 1 if b == 2 else D)
+                add_turned(sums[b][v], term[:, P * v : P * (v + 1)], added[b], count[b])
             added[b] = added[b] + 1
 
-        def gated(b, d, name):
-            term = turns.tile([P, V], F32, name=name, align_bytes=64)
-            gather(b, d, slice(0, V), term[:])
-            add_term(b, term[:])
+        def gather(b, d, targets, picked):
+            window = h[b][:].indirect(pos[d][:, targets.start // 16 : targets.stop // 16])
+            nc.vector.tensor_tensor(picked, window, ratios[d][:, targets], MULT)
 
         def gated_run(b, run, name):
             terms = turns.tile([P, len(run), V], F32, name=name, align_bytes=64)
@@ -268,53 +239,76 @@ def tile_picked_gcn_mlp_none_sub_l_kernel(tc, xT, w1, w2, gate, pos1, pos2, pos3
                 gather(b, d, slice(0, V), terms[:, e, :])
                 add_term(b, terms[:, e, :])
 
+        def gated(b, d, name):
+            gated_run(b, (d,), name)
+
         def plain(b, d, name):
             picked = turns.tile([P, V], F32, name=name, align_bytes=64)
             nc.scalar.activation(picked[:], h[b][:].indirect(pos[d][:]), COPY)
             return picked
+
+        def pivot_term(b, name):
+            add_term(b, plain(b, PIVOT, name)[:])
 
         def weigh(b, d, picked, name):
             term = turns.tile([P, V], F32, name=name, align_bytes=64)
             nc.vector.tensor_tensor(term[:], picked[:], ratios[d], MULT)
             add_term(b, term[:])
 
-        cast_all = turns.tile([P, 10, P, 4], BF16, name="ws0_2", align_bytes=64)
+        scalar_from = PASSES + 2
+        cast_all = turns.tile([P, BLOCKS * PASSES - scalar_from, P, 4], BF16, name="ws0_2", align_bytes=64)
 
-        def cast(b, c, count):
-            slot = PASSES * b + c - 6
-            for e in range(count):
-                interleave(nc.scalar.copy, cast_all[:, slot + e], wraw[b][c + e][:])
-            return cast_all[:, slot : slot + count]
+        def cast_pair(b, c):
+            slot = PASSES * b + c - scalar_from
+            for e in range(2):
+                if b == 2:
+                    nc.scalar.copy(
+                        cast_all[:, slot + e].rearrange("p (u q e) t -> p u q t e", u=2, e=2),
+                        wraw[b][c + e][:].rearrange("p t (q u e) -> p u q t e", u=2, e=2),
+                    )
+                else:
+                    interleave(nc.scalar.copy, cast_all[:, slot + e], wraw[b][c + e][:])
+            return cast_all[:, slot : slot + 2]
 
-        def pivot_term(b, name):
-            add_term(b, plain(b, PIVOT, name)[:])
+        def project(grouped, b, first_pass, name=None):
+            quantise_w1(grouped, b, first_pass, name)
+            if first_pass == 0:
+                hbanks[b] = psum.tile([P, T], F32, name=f"hbank{(b + 1) % 2}")
+            for e in range(grouped.shape[1]):
+                multiply(hbanks[b][:], b, first_pass + e, slice(0, T))
+
+        def keep_h(b, name):
+            h[b] = turns.tile([P, T], F32, name=name, align_bytes=64)
+            nc.scalar.copy(h[b][:], hbanks[b][:])
 
         project(grouped1[:], 1, 0, "wq0_2")
         gated(0, 0, "term00")
         gated(0, 1, "term01")
-        project(cast(1, 2, 2), 1, 2)
+        project(cast_pair(1, 2), 1, 2)
         pivot_term(0, "plain04")
         gated_run(0, (2, 3, 5), "wraw1_3")
-        project(cast(2, 0, 2), 2, 0)
+        project(cast_pair(2, 0), 2, 0)
+
         keep_h(1, "wraw2_1")
         gated(1, 0, "term10")
-        late2 = cast(2, 2, 2)
+        late2 = cast_pair(2, 2)
         gated(1, 1, "wraw2_2")
         project(late2, 2, 2)
         gated(1, 2, "wraw2_3")
-        early3 = cast(3, 0, 2)
+        early3 = cast_pair(3, 0)
         gated(1, 3, "wraw3_0")
         project(early3, 3, 0)
         keep_h(2, "wraw3_1")
         gated(1, 5, "term10")
+
         gated(2, 0, "term20")
-        project(cast(3, 2, 2), 3, 2)
+        project(cast_pair(3, 2), 3, 2)
         gated_run(2, (1, 2, 3), "wraw3_3")
-        p25 = plain(2, 5, "wraw3_2")
+        apart = plain(2, APART, "wraw3_2")
         pivot_term(1, "plain14")
         for v in range(HALVES):
-            nc.tensor.transpose(early[v][:, 2, :], p25[:, P * v : P * (v + 1)], ident[:])
-        keep_h(3, "h3")
+            nc.tensor.transpose(early[v][:, 2, :], apart[:, P * v : P * (v + 1)], ident[:])
+        keep_h(last, "h3")
         pivot_term(2, "plain24")
         for bank in third_banks:
             for nodes in (slice(HT, T), slice(P, HT)):
@@ -327,21 +321,14 @@ def tile_picked_gcn_mlp_none_sub_l_kernel(tc, xT, w1, w2, gate, pos1, pos2, pos3
                     start=True,
                     stop=True,
                 )
-        p33 = plain(3, 3, "plain33")
-        p35 = plain(3, 5, "plain35")
-        gated(3, 0, "term30")
-        gated(3, 1, "wraw3_1")
-        weigh(3, 3, p33, "weighed33")
-        weigh(3, 5, p35, "weighed35")
-        pivot_term(3, "plain34")
 
-        def round_sums(engine, v, first, blocks, bank):
-            to = zT[v][:, :, 32 * first : 32 * (first + blocks), :]
-            sums_v = bank.rearrange("r (q u e) -> r u q e", u=2, e=2)
-            if engine is nc.scalar:
-                nc.scalar.activation(to, sums_v, COPY, scale=pivot[:, v : v + 1])
-            else:
-                nc.vector.tensor_scalar(to, sums_v, pivot[:, v : v + 1], None, MULT)
+        plain33 = plain(last, 3, "plain33")
+        plain35 = plain(last, 5, "plain35")
+        gated(last, 0, "term30")
+        gated(last, 1, "wraw3_1")
+        weigh(last, 3, plain33, "weighed33")
+        weigh(last, 5, plain35, "weighed35")
+        pivot_term(last, "plain34")
 
         zbank = [psum.tile([P, 2, P], F32, name=f"zbank{v}") for v in range(HALVES)]
         zg = [keep.tile([P, P, 4], BF16, name=f"zg{v}", align_bytes=64) for v in range(HALVES)]
@@ -350,10 +337,17 @@ def tile_picked_gcn_mlp_none_sub_l_kernel(tc, xT, w1, w2, gate, pos1, pos2, pos3
         result = [keep.tile([P, P], F32, name=f"result{v}") for v in range(HALVES)]
 
         def gather_half(v):
-            targets = slice(P * v, P * (v + 1))
             term = turns.tile([P, P], F32, name=f"last_term{v}", align_bytes=64)
-            gather(last, 2, targets, term[:])
-            add_turned(last_sums[v][:], term[:], D - 1, D)
+            gather(last, 2, slice(P * v, P * (v + 1)), term[:])
+            add_turned(sums[last][v], term[:], D - 1, D)
+
+        def round_sums(engine, v, first, blocks, bank):
+            to = zT[v][:, :, 32 * first : 32 * (first + blocks), :]
+            sums_v = bank.rearrange("r (q u e) -> r u q e", u=2, e=2)
+            if engine is nc.scalar:
+                nc.scalar.activation(to, sums_v, COPY, scale=pivot[:, v : v + 1])
+            else:
+                nc.vector.tensor_scalar(to, sums_v, pivot[:, v : v + 1], None, MULT)
 
         def turn_back(v):
             words = zT[v][:].rearrange("r u p e -> r (u p e)").bitcast(F32)
@@ -382,19 +376,22 @@ def tile_picked_gcn_mlp_none_sub_l_kernel(tc, xT, w1, w2, gate, pos1, pos2, pos3
         gather_half(0)
         gather_half(1)
         zT = [turns.tile([P, 2, P, 2], BF16, name=n, align_bytes=64) for n in ("plain35", "h3")]
-        scaled = turns.tile([P, HALVES, 2, 32, 2], F32, name="plain33", align_bytes=64)
+        scaled = turns.tile([P, HALVES, P], F32, name="plain33", align_bytes=64)
         for v in range(HALVES):
-            nc.scalar.activation(
-                scaled[:, v], early[v][:, 2, :].rearrange("r (q u e) -> r u q e", u=2, e=2), COPY, scale=weights[:, v, 5:6]
-            )
-        for v, engine in ((1, nc.vector), (0, nc.scalar)):
+            nc.scalar.activation(scaled[:, v], early[v][:, 2, :], COPY, scale=weights[:, v, APART : APART + 1])
+        for v, engine in ((0, nc.scalar), (1, nc.vector)):
             round_sums(engine, v, 0, 2, early[v][:, :2].rearrange("r b c -> r (b c)"))
         for v in range(HALVES):
-            sums_v = third[v].rearrange("r (q u e) -> r u q e", u=2, e=2)
-            for u in range(2):
-                nc.vector.scalar_tensor_tensor(zT[v][:, u, 64:96, :], sums_v[:, u], pivot[:, v : v + 1], scaled[:, v, u], MULT, ADD)
-        round_sums(nc.scalar, 0, last, 1, last_sums[0][:])
-        round_sums(nc.scalar, 1, last, 1, last_sums[1][:])
+            nc.vector.scalar_tensor_tensor(
+                zT[v][:, :, 64:96, :].rearrange("r u q e -> r u (q e)"),
+                sums[2][v].rearrange("r (u x) -> r u x", u=2),
+                pivot[:, v : v + 1],
+                scaled[:, v].rearrange("r (u x) -> r u x", u=2),
+                MULT,
+                ADD,
+            )
+        for v in range(HALVES):
+            round_sums(nc.scalar, v, last, 1, sums[last][v])
         turn_back(0)
         turn_back(1)
         w2g = turns.tile([P, N, 4], BF16, name="last_term1", align_bytes=64)

from contextlib import ExitStack

import concourse.mybir as mybir
from concourse.masks import make_identity

K, T, D, V, H, N = 2048, 512, 6, 256, 512, 128
P = 128
PASSES = K // 512
LAST = PASSES - 1
BLOCKS = H // P
HALVES = V // P
HT = T // 2
FLOPS = 2 * K * H * T + 2 * H * N * V
BYTES = 4 * (K * T + K * H + H * N + D * V + N * V) + 2 * D * P * (V // 16)

SCALAR_COLUMNS_WHOLE = 176
SCALAR_COLUMNS_LAST = (128, 128, 0)
PIVOT = 4
APART = 5
SMALL = 2.0**-30
FLOOR = 2.0**-120

F32 = mybir.dt.float32
BF16 = mybir.dt.bfloat16
U32 = mybir.dt.uint32
U16 = mybir.dt.uint16
U8 = mybir.dt.uint8
FP8X4 = mybir.dt.float8_e4m3fn_x4
MULT = mybir.AluOpType.mult
ADD = mybir.AluOpType.add
MAX = mybir.AluOpType.max
IS_LT = mybir.AluOpType.is_lt
AXIS_X = mybir.AxisListType.X
COPY = mybir.ActivationFunctionType.Copy


def tile_picked_gcn_mlp_none_sub_l_kernel(tc, xT, w1, w2, gate, pos1, pos2, pos3, pos4, pos5, pos6, out):
    nc = tc.nc
    lists_in = (pos1, pos2, pos3, pos4, pos5, pos6)

    with ExitStack() as ctx:
        lists = ctx.enter_context(tc.tile_pool(name="lists", bufs=1))
        keep = ctx.enter_context(tc.tile_pool(name="keep", bufs=1))
        turns = ctx.enter_context(tc.tile_pool(name="turns", bufs=1))
        psum = ctx.enter_context(tc.psum_pool(name="psum", bufs=1))

        pos = [lists.tile([P, V // 16], U16, name=f"pos{d}") for d in range(D)]

        xraw = [turns.tile([P, 4, T], F32, name=f"xraw{c}", align_bytes=64) for c in range(LAST)]
        pieces = [slice(0, HT), slice(HT, HT + P), slice(HT + P, T)]
        xlast = [turns.tile([P, 4, s.stop - s.start], F32, name=f"xlast{a}", align_bytes=64) for a, s in enumerate(pieces)]
        wraw = [[turns.tile([P, 4, P], F32, name=f"wraw{b}_{c}", align_bytes=64) for c in range(PASSES)] for b in range(BLOCKS)]
        w2raw = keep.tile([P, 4, N], F32, name="w2raw")
        gate_rows = turns.tile([P, D // 2, V], F32, name="xg", align_bytes=64)
        nc.gpsimd.memset(gate_rows[: P - 2], 0.0)

        def load_w1(b, c):
            nc.sync.dma_start(
                out=wraw[b][c][:],
                in_=w1[512 * c : 512 * (c + 1), P * b : P * (b + 1)].rearrange("(p j) w -> p j w", j=4),
            )

        def load_list(d):
            nc.sync.dma_start(pos[d][:], lists_in[d])

        load_w1(0, 0)
        nc.sync.dma_start(out=gate_rows[P - 2 :], in_=gate[:, 0, :].rearrange("(g e) v -> e g v", e=2))
        load_w1(0, 1)
        for c in range(LAST):
            nc.sync.dma_start(out=xraw[c][:], in_=xT[512 * c : 512 * (c + 1), :].rearrange("(p j) w -> p j w", j=4))
        load_w1(0, 2)
        load_w1(0, 3)
        for a, nodes in enumerate(pieces):
            nc.sync.dma_start(out=xlast[a][:], in_=xT[512 * LAST :, nodes].rearrange("(p j) w -> p j w", j=4))
        load_w1(1, 0)
        load_w1(1, 1)
        load_w1(1, 2)
        load_list(0)
        load_w1(1, 3)
        for d in (1, PIVOT, 2, 3):
            load_list(d)
        load_w1(2, 0)
        load_list(APART)
        for c in range(1, PASSES):
            load_w1(2, c)
        for c in range(PASSES):
            load_w1(3, c)
        nc.sync.dma_start(out=w2raw[:], in_=w2.rearrange("(p j) m -> p j m", j=4))

        ident = keep.tile([P, P], F32, name="ident")
        make_identity(nc, ident[:])

        gate_cols = keep.tile([P, HALVES, D // 2, 2], F32, name="gate_cols")
        for v in range(HALVES):
            cols_bank = psum.tile([P, D // 2, P], F32, name=f"early{v}")
            for g in range(D // 2):
                nc.tensor.transpose(cols_bank[:, g, :], gate_rows[:, g, P * v : P * (v + 1)], ident[:])
            nc.scalar.copy(gate_cols[:, v], cols_bank[:, :, P - 2 :])
        weights = gate_cols[:].rearrange("r v g e -> r v (g e)")
        top = keep.tile([P, HALVES], F32, name="top")
        size = keep.tile([P, HALVES], F32, name="size")
        bar = keep.tile([P, HALVES], F32, name="bar")
        lift = keep.tile([P, HALVES], F32, name="lift")
        pivot = keep.tile([P, HALVES], F32, name="pivot")
        inverse = keep.tile([P, HALVES], F32, name="inverse")
        ratio_cols = keep.tile([P, HALVES, D], F32, name="ratio_cols")
        nc.vector.tensor_reduce(top[:], weights, AXIS_X, MAX, apply_absolute_value=True)
        nc.vector.scalar_tensor_tensor(size[:], weights[:, :, PIVOT], -1.0, weights[:, :, PIVOT], MULT, MAX)
        nc.vector.tensor_scalar(bar[:], top[:], SMALL, FLOOR, MULT, MAX)
        for v in range(HALVES):
            one = slice(v, v + 1)
            nc.vector.scalar_tensor_tensor(lift[:, one], size[:, one], bar[:, one], bar[:, one], IS_LT, MULT)
        nc.vector.scalar_tensor_tensor(pivot[:], lift[:], 2.0, weights[:, :, PIVOT], MULT, ADD)
        nc.vector.reciprocal(inverse[:], pivot[:])
        for v in range(HALVES):
            nc.vector.tensor_scalar(ratio_cols[:, v], weights[:, v], inverse[:, v : v + 1], None, MULT)
        gate_banks = []
        for pair, name in (((0, 1), "zbank1"), ((2, 3), "last0"), ((APART,), "last1")):
            pair_bank = psum.tile([P, len(pair), V], F32, name=name)
            for e, d in enumerate(pair):
                for v in range(HALVES):
                    nc.tensor.transpose(
                        pair_bank[:, e, v * P : (v + 1) * P], ratio_cols[:, v, d : d + 1].to_broadcast([P, P]), ident[:]
                    )
            gate_banks.append((pair, pair_bank))

        ratios = {}

        def keep_gates(first, stop, name):
            count = sum(len(pair) for pair, bank in gate_banks[first:stop])
            kept = turns.tile([P, count, V], F32, name=name, align_bytes=64)
            at = 0
            for pair, bank in gate_banks[first:stop]:
                nc.scalar.copy(kept[:, at : at + len(pair)], bank[:])
                for e, d in enumerate(pair):
                    ratios[d] = kept[:, at + e]
                at = at + len(pair)

        def interleave(copy, grouped, raw):
            copy(grouped.rearrange("p (c i) t -> p c t i", i=4), raw.rearrange("p t (c i) -> p c t i", i=4))

        wq = {}
        xq = [
            (
                keep.tile([P, T], U32, name=f"xq{c}", align_bytes=64),
                keep.tile([P, T], U8, name=f"xs{c}", align_bytes=64),
            )
            for c in range(PASSES)
        ]
        h = {}

        def quantise_w1(grouped, b, first_pass, name=None):
            count = grouped.shape[1]
            codes = turns.tile([P, count, P], U32, name=name or f"wq{b}_{first_pass}", align_bytes=64)
            scales = turns.tile([P, count, P], U8, name=f"ws{b}_{first_pass}", align_bytes=64)
            nc.vector.quantize_mx(
                out=codes[:].rearrange("p c w -> p (c w)").bitcast(FP8X4),
                scales=scales[:].rearrange("p c w -> p (c w)"),
                in_=grouped.rearrange("p c w t -> p (c w t)"),
            )
            for e in range(count):
                wq[b, first_pass + e] = (codes[:, e, :], scales[:, e, :])

        def quantise_x(c, raw, nodes, cut, name):
            grouped = turns.tile([P, nodes.stop - nodes.start, 4], BF16, name=name, align_bytes=64)
            if cut > 0:
                interleave(nc.scalar.copy, grouped[:, :cut, :], raw[:, :, :cut])
            if cut < nodes.stop - nodes.start:
                interleave(nc.vector.tensor_copy, grouped[:, cut:, :], raw[:, :, cut:])
            nc.vector.quantize_mx(
                out=xq[c][0][:, nodes].bitcast(FP8X4), scales=xq[c][1][:, nodes], in_=grouped[:].rearrange("p w t -> p (w t)")
            )

        def multiply(bank, b, c, nodes):
            nc.tensor.matmul_mx(
                out=bank,
                lhsT=wq[b, c][0].bitcast(FP8X4),
                lhsT_scale=wq[b, c][1],
                rhs=xq[c][0][:, nodes].bitcast(FP8X4),
                rhs_scale=xq[c][1][:, nodes],
                start=(c == 0),
                stop=(c == LAST),
            )

        grouped = turns.tile([P, 2, P, 4], BF16, name="grouped0_0", align_bytes=64)
        for c in range(2):
            interleave(nc.vector.tensor_copy, grouped[:, c], wraw[0][c][:])
        quantise_w1(grouped[:], 0, 0)
        first_banks = [psum.tile([P, s.stop - s.start], F32, name=n) for s, n in zip(pieces, ("hbank0", "hbank1", "zbank0"))]
        for c in range(LAST):
            quantise_x(c, xraw[c], slice(0, T), SCALAR_COLUMNS_WHOLE, "xg")
            if c == 1:
                keep_gates(0, 2, "xraw1")
            if c == 2:
                grouped = turns.tile([P, 2, P, 4], BF16, name=f"xraw{c}", align_bytes=64)
                interleave(nc.scalar.copy, grouped[:, 0], wraw[0][2][:])
                interleave(nc.vector.tensor_copy, grouped[:, 1], wraw[0][3][:])
                quantise_w1(grouped[:], 0, 2)
            for bank, nodes in zip(first_banks, pieces):
                multiply(bank[:], 0, c, nodes)
        for a, name in enumerate(("xg", "xlast0", "xg")):
            quantise_x(LAST, xlast[a], pieces[a], SCALAR_COLUMNS_LAST[a], name)
            multiply(first_banks[a][:], 0, LAST, pieces[a])
        keep_gates(2, 3, "xlast1")
        grouped1 = turns.tile([P, 2, P, 4], BF16, name="xlast2", align_bytes=64)
        interleave(nc.vector.tensor_copy, grouped1[:, 0], wraw[1][0][:])
        interleave(nc.vector.tensor_copy, grouped1[:, 1], wraw[1][1][:])
        h[0] = turns.tile([P, T], F32, name="h0", align_bytes=64)
        for copy, bank, nodes in zip((nc.scalar.copy, nc.scalar.copy, nc.vector.tensor_copy), first_banks, pieces):
            copy(h[0][:, nodes], bank[:])

        w2s = keep.tile([P, N], U8, name="w2s", align_bytes=64)

        early = [psum.tile([P, 3, P], F32, name=f"early{v}") for v in range(HALVES)]
        third_banks = [psum.tile([P, T], F32, name=f"zbank{v}") for v in range(HALVES)]
        last = BLOCKS - 1
        last_banks = [psum.tile([P, P], F32, name=f"last{v}") for v in range(HALVES)]
        sums = [[early[v][:, b, :] for v in range(HALVES)] for b in range(2)]
        sums = sums + [[bank[:, :P] for bank in third_banks], [bank[:] for bank in last_banks]]
        count = (D, D, D - 1, D)
        added = [0] * BLOCKS
        hbanks = {}

        def add_turned(acc, picked, place, terms):
            nc.tensor.matmul(acc, picked, ident[:], is_transpose=True, start=(place == 0), stop=(place == terms - 1))

        def add_term(b, term):
            for v in range(HALVES):
                add_turned(sums[b][v], term[:, P * v : P * (v + 1)], added[b], count[b])
            added[b] = added[b] + 1

        def gather(b, d, targets, picked):
            window = h[b][:].indirect(pos[d][:, targets.start // 16 : targets.stop // 16])
            nc.vector.tensor_tensor(picked, window, ratios[d][:, targets], MULT)

        def gated_run(b, run, name):
            terms = turns.tile([P, len(run), V], F32, name=name, align_bytes=64)
            for e, d in enumerate(run):
                gather(b, d, slice(0, V), terms[:, e, :])
                add_term(b, terms[:, e, :])

        def gated(b, d, name):
            gated_run(b, (d,), name)

        def plain(b, d, name):
            picked = turns.tile([P, V], F32, name=name, align_bytes=64)
            nc.scalar.activation(picked[:], h[b][:].indirect(pos[d][:]), COPY)
            return picked

        def pivot_term(b, name):
            add_term(b, plain(b, PIVOT, name)[:])

        def weigh(b, d, picked, name):
            term = turns.tile([P, V], F32, name=name, align_bytes=64)
            nc.vector.tensor_tensor(term[:], picked[:], ratios[d], MULT)
            add_term(b, term[:])

        scalar_from = PASSES + 2
        cast_all = turns.tile([P, BLOCKS * PASSES - scalar_from, P, 4], BF16, name="ws0_2", align_bytes=64)

        def cast_pair(b, c):
            slot = PASSES * b + c - scalar_from
            for e in range(2):
                if b == 2:
                    nc.scalar.copy(
                        cast_all[:, slot + e].rearrange("p (u q e) t -> p u q t e", u=2, e=2),
                        wraw[b][c + e][:].rearrange("p t (q u e) -> p u q t e", u=2, e=2),
                    )
                else:
                    interleave(nc.scalar.copy, cast_all[:, slot + e], wraw[b][c + e][:])
            return cast_all[:, slot : slot + 2]

        def project(grouped, b, first_pass, name=None):
            quantise_w1(grouped, b, first_pass, name)
            if first_pass == 0:
                hbanks[b] = psum.tile([P, T], F32, name=f"hbank{(b + 1) % 2}")
            for e in range(grouped.shape[1]):
                multiply(hbanks[b][:], b, first_pass + e, slice(0, T))

        def keep_h(b, name):
            h[b] = turns.tile([P, T], F32, name=name, align_bytes=64)
            nc.scalar.copy(h[b][:], hbanks[b][:])

        project(grouped1[:], 1, 0, "wq0_2")
        gated(0, 0, "term00")
        gated(0, 1, "term01")
        project(cast_pair(1, 2), 1, 2)
        pivot_term(0, "plain04")
        gated_run(0, (2, 3, 5), "wraw1_3")
        project(cast_pair(2, 0), 2, 0)

        keep_h(1, "wraw2_1")
        gated(1, 0, "term10")
        late2 = cast_pair(2, 2)
        gated(1, 1, "wraw2_2")
        project(late2, 2, 2)
        gated(1, 2, "wraw2_3")
        early3 = cast_pair(3, 0)
        gated(1, 3, "wraw3_0")
        project(early3, 3, 0)
        keep_h(2, "wraw3_1")
        gated(1, 5, "term10")

        gated(2, 0, "term20")
        project(cast_pair(3, 2), 3, 2)
        gated_run(2, (1, 2, 3), "wraw3_3")
        apart = plain(2, APART, "wraw3_2")
        pivot_term(1, "plain14")
        for v in range(HALVES):
            nc.tensor.transpose(early[v][:, 2, :], apart[:, P * v : P * (v + 1)], ident[:])
        keep_h(last, "h3")
        pivot_term(2, "plain24")
        for bank in third_banks:
            for nodes in (slice(HT, T), slice(P, HT)):
                nc.tensor.matmul_mx(
                    out=bank[:, nodes],
                    lhsT=wq[last, LAST][0].bitcast(FP8X4),
                    lhsT_scale=wq[last, LAST][1],
                    rhs=xq[LAST][0][:, nodes].bitcast(FP8X4),
                    rhs_scale=xq[LAST][1][:, nodes],
                    start=True,
                    stop=True,
                )

        plain33 = plain(last, 3, "plain33")
        plain35 = plain(last, 5, "plain35")
        gated(last, 0, "term30")
        gated(last, 1, "wraw3_1")
        weigh(last, 3, plain33, "weighed33")
        weigh(last, 5, plain35, "weighed35")
        pivot_term(last, "plain34")

        zbank = [psum.tile([P, 2, P], F32, name=f"zbank{v}") for v in range(HALVES)]
        zg = [keep.tile([P, P, 4], BF16, name=f"zg{v}", align_bytes=64) for v in range(HALVES)]
        zq = [keep.tile([P, P], U32, name=f"zq{v}", align_bytes=64) for v in range(HALVES)]
        zs = [keep.tile([P, P], U8, name=f"zs{v}", align_bytes=64) for v in range(HALVES)]
        result = [keep.tile([P, P], F32, name=f"result{v}") for v in range(HALVES)]

        def gather_half(v):
            term = turns.tile([P, P], F32, name=f"last_term{v}", align_bytes=64)
            gather(last, 2, slice(P * v, P * (v + 1)), term[:])
            add_turned(sums[last][v], term[:], D - 1, D)

        def round_sums(engine, v, first, blocks, bank):
            to = zT[v][:, :, 32 * first : 32 * (first + blocks), :]
            sums_v = bank.rearrange("r (q u e) -> r u q e", u=2, e=2)
            if engine is nc.scalar:
                nc.scalar.activation(to, sums_v, COPY, scale=pivot[:, v : v + 1])
            else:
                nc.vector.tensor_scalar(to, sums_v, pivot[:, v : v + 1], None, MULT)

        def turn_back(v):
            words = zT[v][:].rearrange("r u p e -> r (u p e)").bitcast(F32)
            for u in range(2):
                nc.tensor.transpose(zbank[v][:, u, :], words[:, P * u : P * (u + 1)], ident[:])
            nc.scalar.copy(
                zg[v][:].rearrange("p r t -> p (r t)").bitcast(F32).rearrange("p (r u) -> p r u", u=2),
                zbank[v][:].rearrange("p u r -> p r u"),
            )

        def second_layer(v, copy):
            nc.vector.quantize_mx(out=zq[v][:].bitcast(FP8X4), scales=zs[v][:], in_=zg[v][:].rearrange("p r t -> p (r t)"))
            bank = psum.tile([P, P], F32, name=f"hbank{v}")
            nc.tensor.matmul_mx(
                out=bank[:],
                lhsT=w2q[:].bitcast(FP8X4),
                lhsT_scale=w2s[:],
                rhs=zq[v][:].bitcast(FP8X4),
                rhs_scale=zs[v][:],
                start=True,
                stop=True,
            )
            copy(result[v][:], bank[:])
            nc.sync.dma_start(out=out[:, P * v : P * (v + 1)], in_=result[v][:])

        gather_half(0)
        gather_half(1)
        zT = [turns.tile([P, 2, P, 2], BF16, name=n, align_bytes=64) for n in ("plain35", "h3")]
        scaled = turns.tile([P, HALVES, P], F32, name="plain33", align_bytes=64)
        for v in range(HALVES):
            nc.scalar.activation(scaled[:, v], early[v][:, 2, :], COPY, scale=weights[:, v, APART : APART + 1])
        for v, engine in ((0, nc.scalar), (1, nc.vector)):
            round_sums(engine, v, 0, 2, early[v][:, :2].rearrange("r b c -> r (b c)"))
        for v in range(HALVES):
            nc.vector.scalar_tensor_tensor(
                zT[v][:, :, 64:96, :].rearrange("r u q e -> r u (q e)"),
                sums[2][v].rearrange("r (u x) -> r u x", u=2),
                pivot[:, v : v + 1],
                scaled[:, v].rearrange("r (u x) -> r u x", u=2),
                MULT,
                ADD,
            )
        for v in range(HALVES):
            round_sums(nc.scalar, v, last, 1, sums[last][v])
        turn_back(0)
        turn_back(1)
        w2g = turns.tile([P, N, 4], BF16, name="last_term1", align_bytes=64)
        interleave(nc.vector.tensor_copy, w2g[:], w2raw[:])
        w2q = turns.tile([P, N], U32, name="w2q", align_bytes=64)
        nc.vector.quantize_mx(out=w2q[:].bitcast(FP8X4), scales=w2s[:], in_=w2g[:].rearrange("p m t -> p (m t)"))
        second_layer(0, nc.scalar.copy)
        second_layer(1, nc.vector.tensor_copy)
